import numpy as np, ml_dtypes
CORES = [25,29,65,69,153,157,193,197]
N = 8
BF = ml_dtypes.bfloat16
W, S, M, CAP, RO, DX = 4096, 1024, 12, 48, 3, 4
def places(g, w, k):
    u = np.add.reduce(w[..., :, None] * g, axis=-2) & 4095
    return ((u * u >> 5)[..., None, :] + k[..., :, None] * u[..., None, :]) & (W - 1)
def parts(rng):
    return (rng.integers(0, 256, (N, 8, 16, W), dtype=np.int32), rng.integers(0, 256, (N, 8, 16, S)), rng.integers(0, 256, (N, 8, 16, RO)),
            rng.integers(0, 3969, (N, 8, M)), rng.integers(620, 1000, (N, 8)))
def pack(x, g, w, k, t):
    return {"xs": x.reshape(N, 128, W).astype(np.float32).astype(BF), "gd": g.reshape(N, 128, S).astype(np.float32).astype(BF), "wt": w.reshape(N, 128, RO).astype(np.int32),
            "km": np.repeat(k, 16, axis=1).astype(np.int32), "th": np.repeat(t, 16, axis=1)[:, :, None].astype(np.int32)}
def plant(x, g, j, c, i, d):
    v = 255 - g[:, j]; n = np.arange(len(j)); a = v[i, n]
    v[i, n] = np.where(a < 128, a + d, a - d); x[:, c] = v
def lone(rng, x, g, w, k, s0, s1, lo, hi):
    c = places(g, w, k)[:, s0:s1]; m, j = np.nonzero((c >= lo) & (c < hi))
    if len(m):
        i = int(rng.integers(0, len(m))); x[:, c[m[i], j[i]]] = 255 - g[:, s0 + j[i]]
def setup_inputs(rng):
    x, g, w, k, t = parts(rng); h = rng.integers(0, 8)
    t[0, h] = 995; t[1, h] = 620; t[DX, h] = 620
    return pack(x, g, w, k, t)
def setup_inputs_room(rng):
    x, g, w, k, t = parts(rng); t = rng.integers(60, 129, (N, 8)); k = np.minimum(k | 1, 3967)
    for q in range(N):
        room = rng.permutation(np.array([0, 1, CAP - 1, CAP, CAP + 1, 2 * CAP, 0, CAP]))
        for h in range(8):
            c = places(g[q, h], w[q, h, :, 0], k[q, h])[rng.integers(0, M, S), np.arange(S)]
            o = rng.permutation(S); o = o[c[o] < W - 96]; first = np.unique(c[o], return_index=True)[1]
            o = o[np.sort(first)][:int(room[h])]; n = len(o)
            plant(x[q, h], g[q, h], o, c[o], rng.integers(0, 16, n), rng.integers(0, t[q, h], n))
    return pack(x, g, w, k, t)
def setup_inputs_ties(rng):
    x, g, w, k, t = parts(rng)
    w[:, :, 2, 0] = w[:, :, 1, 0]; g[:, :, 1] = np.minimum(g[:, :, 1], 254); g[:, :, 2] = np.maximum(g[:, :, 2], 1)
    for q in range(N):
        for h in (0, 2, 4, 6):
            n = int(rng.choice(np.array([CAP // 4, CAP // 2, CAP]))); t[q, h] = 3 if h == 2 * (q % 4) else rng.integers(1, 4)
            o = rng.permutation(S); a = np.minimum(o[:n], o[n:2 * n]); b = np.maximum(o[:n], o[n:2 * n]); e = o[2 * n:3 * n]
            kd = rng.integers(0, 4, n); kd[:4] = np.arange(4); s = (kd > 0).astype(np.int64)
            v = g[q, h][:, a].copy(); v[1] += s; v[2] -= s; g[q, h][:, b] = v
            c = places(g[q, h], w[q, h, :, 0], k[q, h])
            ca = c[rng.integers(0, M, n), a]; m = rng.integers(0, M, n); c1 = c[m, e]; c2 = c[(m + rng.integers(1, M, n)) % M, e]
            al = np.concatenate([ca, c1, c2]); one = np.bincount(al, minlength=W)[al] == 1
            pa = one[:n] & (ca < W - 96); pe = one[n:2 * n] & one[2 * n:]
            v = 255 - g[q, h][:, a]; v[1] -= ((kd == 1) | (kd == 2)).astype(np.int64); v[2] += (kd == 1).astype(np.int64); x[q, h][:, ca[pa]] = v[:, pa]
            i = rng.integers(0, 16, n); d = rng.integers(0, t[q, h], n)
            plant(x[q, h], g[q, h], e[pe], c1[pe], i[pe], d[pe]); plant(x[q, h], g[q, h], e[pe], c2[pe], i[pe], d[pe])
    a = int(rng.integers(0, S // 4)); b = a + int(rng.integers(1, S // 4))
    w[:, 1, :, 0] = 0; w[:, 1, 0, 0] = 1; k[:, 1, 0] = 0; k[:, 1, 1] = 3; t[:, 1] = 20
    g[:, 1, :, b] = g[:, 1, :, a].copy(); g[:, 1, 0, a] = 32; g[:, 1, 0, b] = 64
    x[:, 1, :, 128] = 255 - g[:, 1, :, a]; x[:, 1, 0, 128] = 207
    return pack(x, g, w, k, t)
def setup_inputs_ends(rng):
    x, g, w, k, t = parts(rng); o = rng.permutation(8); w[:, :, 0, 0] |= 1
    low = rng.integers(0, 192, (N, 4, W)); few = rng.integers(0, 64, (N, W)) == 0
    x[:, o[0], 0] = low[:, 0]; x[:, o[1], 0] = rng.integers(192, 256, (N, W))
    x[:, o[2], 0] = low[:, 1]; x[:, o[2], 0, 0] = 192; x[::2, o[2], 0, W - 1] = 255
    x[1::2, o[2], 0, W - 40] = 192; x[1::2, o[2], 0, W - 20] = 192
    x[:, o[3], 0, W // 2:] = low[:, 2, W // 2:]; x[:, o[4], 0] = np.where(few, 192, low[:, 3])
    x[:, o[6], 0, W - 81:] = low[:, 0, W - 81:]; x[:, o[7], 0, W - 81:] = low[:, 1, W - 81:]; x[:, o[7], 0, W - 4] = 192
    t[::2, o[0]] = 4080; t[1::2, o[0]] = 4; t[1::2, o[2]] = 4
    for q in range(1, N, 2):
        lone(rng, x[q, o[0]], g[q, o[0]], w[q, o[0], :, 0], k[q, o[0]], 0, S // 4, W // 2, W - 96)
        lone(rng, x[q, o[0]], g[q, o[0]], w[q, o[0], :, 1], k[q, o[0]], S // 4, S - 3 * CAP, 0, W // 4)
        lone(rng, x[q, o[2]], g[q, o[2]], w[q, o[2], :, 0], k[q, o[2]], 0, S, 0, W // 4)
    for q in range(N):
        for h in o[5:]:
            u = np.add.reduce(w[q, h, :, 0][:, None] * g[q, h], axis=0) & 4095; used = []
            for m, c in enumerate((W - 97, W - 96, 0)):
                for j in range(S):
                    if u[j] & 1 and j not in used:
                        v = int(u[j]); kk = (c - (v * v >> 5)) * pow(v, -1, W) % W
                        if kk <= 3968:
                            k[q, h, m] = kk; used.append(j)
                            plant(x[q, h], g[q, h], np.array([j]), np.array([c]), np.array([3 + m]), np.array([m])); break
    return pack(x, g, w, k, t)
def setup_inputs_alike(rng):
    x, g, w, k, t = parts(rng); o = rng.permutation(8)
    g[:, o[0]] = g[:, o[0], :, :1].copy()
    for q in range(N):
        c = places(g[q, o[0]], w[q, o[0], :, 0], k[q, o[0]])[:, 0]; m = np.flatnonzero(c < W - 96)[:1]
        plant(x[q, o[0]], g[q, o[0]], np.zeros(len(m), np.int64), c[m], m, np.full(len(m), 3))
    w[:, o[1]] = 0
    for q in range(N):
        e = np.arange(1, CAP + 1); d = np.append(e[::-1] if q % 2 == 0 else e, 0); n = np.arange(CAP + 1); i = rng.integers(0, 16, CAP + 1)
        v = np.repeat(255 - x[q, o[1], :, :1], CAP + 1, axis=1); a = v[i, n]
        v[i, n] = np.where(a < 128, a + d, a - d); g[q, o[1], :, :CAP + 1] = v
    k[:, o[2]] = k[:, o[2], :1].copy()
    g[:, o[3]] = g[:, o[3]][:, :, rng.integers(0, 4, S)]
    b = x[:, o[4], :, :8].copy(); b[:, 0, 0] = 200
    x[:, o[4]] = b[:, :, rng.integers(0, 8, W)]; g[:, o[4]] = 255 - b[:, :, rng.integers(0, 8, S)]
    k[:, o[5]] = rng.choice(np.array([0, 1, 3968]), (N, M))
    x[:, o[6]] = 255 * rng.integers(0, 2, (N, 16, W)); g[:, o[6]] = 255 * rng.integers(0, 2, (N, 16, S))
    w[:, o[7], :, 0] = 0; w[:, o[7], 0, 0] = 1; k[:, o[7]] = rng.integers(0, 8, (N, M)); t[:, o[7]] = 4080
    g[:, o[7], 0] = np.minimum(g[:, o[7], 0], 254); g[:, o[7], 0, S - 1] = 255
    for q in range(N):
        c = int(places(g[q, o[7]], w[q, o[7], :, 0], k[q, o[7]])[0, S - 1]); x[q, o[7], :, c] = 255 - g[q, o[7], :, S - 1]
    return pack(x, g, w, k, t)
def setup_inputs_spread(rng):
    x, g, w, k, t = parts(rng)
    def uneven(n):
        v = np.minimum((np.exp2(8 * rng.random((N, 8, 1, n))) * rng.random((N, 8, 16, n))).astype(np.int64), 255)
        return np.where(rng.random((N, 8, 1, n)) < 0.5, v, 255 - v)
    x = uneven(W); g = uneven(S)
    w = np.minimum(np.exp2(8 * rng.random(w.shape)).astype(np.int64), 255); k = np.minimum(np.exp2(12 * rng.random(k.shape)).astype(np.int64), 3968)
    t = np.minimum(np.maximum(np.exp2(12 * rng.random((N, 8))).astype(np.int64), 1), 4080); t[:, rng.integers(0, 8)] = rng.integers(1500, 2500, N)
    return pack(x, g, w, k, t)
def check_inputs(d):
    bad = []
    for n, lo, hi in (("xs", 0, 255), ("gd", 0, 255), ("wt", 0, 255), ("km", 0, 3968), ("th", 1, 4080)):
        a = np.asarray(d[n]).astype(np.float64)
        if not np.all((a >= lo) & (a <= hi) & (np.floor(a) == a)): bad.append("range of " + n)
    for n in ("km", "th"):
        a = np.asarray(d[n]).reshape(N, 8, 16, -1)
        if np.any(a != a[:, :, :1]): bad.append("rows of a group alike in " + n)
    return bad
def reference(xs, gd, wt, km, th):
    x = xs.astype(np.float32).astype(np.int32).reshape(N, 8, 16, W); g = gd.astype(np.float32).astype(np.int32).reshape(N, 8, 16, S)
    w = wt.astype(np.int64).reshape(N, 8, 16, RO); k = km.astype(np.int64).reshape(N, 8, 16, M)[:, :, 0]; t = th.astype(np.int64).reshape(N, 8, 16)[:, :, 0]
    log = np.zeros((N, 8, W), np.int64); place = np.arange(W); slot = np.arange(S); rows = np.arange(8)[:, None]
    for rnd in range(RO):
        cuts = []; gives = []; nx = []
        for a in range(N):
            c = places(g[a], w[a, :, :, rnd], k[a])
            v = np.take_along_axis(x[a], c.reshape(8, 1, M * S), 2).reshape(8, 16, M, S)
            D = np.add.reduce(np.abs(g[a][:, :, None, :] + v - 255), axis=1)
            m = np.argmin(D, axis=1)[:, None]
            D = np.take_along_axis(D, m, 1)[:, 0].astype(np.int64); c = np.take_along_axis(c, m, 1)[:, 0]
            fit = (D < t[a][:, None]) & (c < W - 96)
            cand = fit & (np.add.accumulate(fit.astype(np.int64), axis=1) <= CAP)
            key = D * S + slot; low = np.full((8, W), 2 ** 40, np.int64)
            np.minimum.at(low, (rows, c), np.where(cand, key, 2 ** 40))
            cut = cand & (np.take_along_axis(low, c, 1) == key)
            ok = (x[a][:, 0] >= 192) & (x[a][:, 0] <= 255)
            U = np.minimum.accumulate(np.where(ok, place, W - 1)[:, ::-1], axis=1)[:, ::-1]
            e1 = np.take_along_axis(U, np.minimum(c + 16, W - 1), 1); e2 = np.take_along_axis(U, np.minimum(e1 + 8, W - 1), 1)
            gives.append([np.maximum(255 - np.take_along_axis(x[a], e[:, None, :], 2), 0) for e in (np.minimum(c + 10, W - 1), e1, e2)])
            reach = np.full((8, W), -1, np.int64); np.maximum.at(reach, (rows, c), np.where(cut, e2, -1))
            gone = np.maximum.accumulate(reach, axis=1) >= place
            log[a] = np.where(gone & (log[a] == 0), rnd + 1, log[a])
            nx.append(np.where(gone[:, None, :], np.int32(512), x[a])); cuts.append(cut)
        ng = []
        for a in range(N):
            p, q = a ^ 1, a ^ DX
            every = np.concatenate([gives[p][0], gives[q][1], gives[q][2], g[a], g[a]], axis=2)
            there = np.concatenate([cuts[p], cuts[q], cuts[q], ~cuts[a], cuts[a]], axis=1)
            o = np.argsort(~there, axis=1, kind="stable")[:, :S]
            ng.append(np.take_along_axis(every, o[:, None, :], 2))
        x = np.stack(nx); g = np.stack(ng)
    return {"yg": g.reshape(N, 128, S).astype(np.float32).astype(BF), "yc": log.astype(np.float32)}

@@ -1,0 +1,635 @@
+from concourse.bass import DstId, RemoteDMATransfer
+from concourse.mybir import AluOpType as Op, AxisListType, ActivationFunctionType as Fn
+
+RO, M, S, W, CAP = 3, 12, 1024, 4096, 48
+POOLW = 192 + S + 240
+_F32 = """wf 3 KF 12 TH 1 KD 1 SW 3 Pf 1 PI 1 PG 1 P16 1 P256 1 BF 128 tA 128 tB 128 tC 128 tD 128 tE 128 WM 96 R48 48 RI 48 SLW 80 RBH 3 RC 3
+ PL 256 BM 16 EG 4 ZER 64 uf 64 Q 80 cur 192 fa 64 Cs 64 junk 192 sA 3 OH 48 M1 192 xk 48 US 144 tk 48 RV 48 vl 3 CKm 96 SLm 48 cw 3 kw 3 sw 3
+ tm 144 mn 3 eq 3 vv 3 nc 3 n5 3 pv 3 sel 48 T1 48 em 48 ew 6 UT 256 TU 256 fw 16 nf 1 wt4 1 CF 12 PO 4 ac 3 PF 4 lf 64
+ yct 256 YB 3 CN 3 CNL 6"""
+_BF = """X 4096 GL 1024 YG 1024 Z 12288 A 12288 wb 3 Z1 144 Z64 144 Z128 144 ZN 144 ZW 432 B 128 NB 128 ID 128 NI 128 TN 128 TS 128 TQ 128
+ B0 128 TG 128 Y3 128 Y1 128 AG 128 AGp 128 IO16 64 IO 256 BI 768 C2 768 FB 64 CB 8 GX 144 GN 144 GV 144 LH 1024 RH 1536 lc 1 R0 256 NK 256
+ tg 48 SND 1152 POOL 4368"""
+_I32 = """wi 3 ki 12 ti 1 IP 1 IPa 1 IPb 1 IQ 144 IQa 128 IQb 128 IZ 144 IJ 80 I256 256 WI 96 UW 80 FW 80 KW 80 u0 64 f0 64 CI 768 CM 768
+ fb 64 kI 48 mI 48 dm 48 ts 48 CK 96 p1 48 p1h 48 q1 3 q1l 3 CE 18 PJ 8"""
+_U16 = "CL 768 sO 4 DL 12 OFF 12 qO 4 LST 64 sl16 4"
+COLS, SCRATCH, PLACE = {}, {}, {}
+for _txt, _dt in ((_F32, "float32"), (_BF, "bfloat16"), (_I32, "int32"), (_U16, "uint16")):
+    _w, _at = _txt.split(), 16
+    for _k in range(0, len(_w), 2):
+        _n = int(_w[_k + 1])
+        COLS[_w[_k]] = _n
+        if _dt == "bfloat16" or _w[_k] in ("CN", "CNL"):
+            SCRATCH[_w[_k]] = ("sbuf", [128, _n], _dt)
+        else:
+            PLACE[_w[_k]] = ("all_" + _dt, _at)
+            _at += _n + (-_n) % 16
+    if _dt != "bfloat16":
+        SCRATCH["all_" + _dt] = ("sbuf", [128, _at], _dt)
+for _b in range(8):
+    SCRATCH["P%d" % _b] = ("psum", [128, 512], "float32")
+    COLS["P%d" % _b] = 512
+LOADS = ["dG", "dW", "dK", "dT", "dX", "dX2", "dR", "dM0", "dM1", "dY0", "dY1", "dC"]
+SEMAPHORES = ["sV", "sS", "sP", "sG", "lsem", "cn0", "cn1", "cn2", "ar0", "ar1", "ar2"] + LOADS
+
+SMS = (0, 1, 3, 6)
+RMS = (9, 10, 11)
+
+
+def R(b, lo=0, hi=None):
+    return (b, lo, COLS[b] if hi is None else hi)
+
+
+def reg(x):
+    if not isinstance(x, str):
+        return x
+    p = x.split(":")
+    lo = int(p[1]) if len(p) > 1 else 0
+    return (p[0], lo, int(p[2]) if len(p) > 2 else lo + 1 if len(p) > 1 else COLS[p[0]])
+
+
+def sub(r, lo, hi):
+    return (r[0], r[1] + lo, r[1] + hi)
+
+
+WAKE, CYC, GATHER, SLACK = 0.12, 1.04e-3, 1.5, 0.10
+HINT = ("04063769656271386045144780815589920545733890020253425010900001080800440909354774405107808900080800275990981087050920792303210856000859"
+        "020324062016193719011460005540009729252008968738078207900107450755950678724219169209800513049000919002101803720839245550202005003002061")
+TWO = {_k for _t in (_BF, _U16) for _k in _t.split()}
+ORDERS = {}
+
+
+def psum(b):
+    return b[0] == "P" and b[1:] in "01234567" and len(b) == 2
+
+
+def plan(nodes):
+    n, hist = len(nodes), {}
+    pre, suc = [set() for _ in nodes], [[] for _ in nodes]
+    for i, x in enumerate(nodes):
+        for regs, wr in ((x["rd"], False), (x["wr"], True)):
+            for b, lo, hi in regs:
+                for l, h, w, j, q in hist.get(b, ()):
+                    if (l < hi and lo < h and (w or wr)) or (psum(b) and q != x["q"]):
+                        pre[i].add(j)
+        pre[i].update(x["dep"])
+        pre[i].discard(i)
+        for regs, wr in ((x["rd"], False), (x["wr"], True)):
+            for b, lo, hi in regs:
+                h = hist.setdefault(b, [])
+                if wr and not psum(b):
+                    h[:] = [e for e in h if not (lo <= e[0] and e[1] <= hi)]
+                h.append((lo, hi, wr, i, x["q"]))
+        for j in pre[i]:
+            suc[j].append(i)
+    prio = [0.0] * n
+    for i in range(n - 1, -1, -1):
+        prio[i] = nodes[i]["dur"] + nodes[i]["lat"] + max([prio[j] + WAKE for j in suc[i]], default=0.0)
+    prio = [p + 0.5 * int(HINT[x["key"]]) if 0 <= x["key"] < len(HINT) else p for p, x in zip(prio, nodes)]
+    left, rdy = [len(p) for p in pre], [0.0] * n
+    ready, free, order = {}, {}, []
+    for i in range(n):
+        if not left[i]:
+            ready.setdefault(nodes[i]["q"], []).append(i)
+    while len(order) < n:
+        best = None
+        for q, l in ready.items():
+            if not l:
+                continue
+            f = free.get(q, 0.0)
+            t = min(max(f, rdy[i]) for i in l) + SLACK
+            i = max((i for i in l if max(f, rdy[i]) <= t), key=lambda i: (prio[i], -i))
+            s = max(f, rdy[i])
+            if best is None or s < best[0]:
+                best = (s, q, i)
+        s, q, i = best
+        ready[q].remove(i)
+        order.append(i)
+        if q != "R":
+            free[q] = s + nodes[i]["dur"]
+        end = s + nodes[i]["dur"] + nodes[i]["lat"] + WAKE
+        for j in suc[i]:
+            rdy[j] = max(rdy[j], end)
+            left[j] -= 1
+            if not left[j]:
+                ready.setdefault(nodes[j]["q"], []).append(j)
+    return order
+
+
+def builder(g, T):
+    eng = {"V": g.vector, "S": g.scalar, "P": g.tensor, "G": g, "Y": g.sync}
+    cnt = {"V": 0, "S": 0, "P": 0, "G": 0}
+    know = {q: {} for q in eng}
+    snap = {}
+    hist = {}
+    nodes, key = [], [0]
+
+    def wait(q, reads, writes):
+        want = {}
+        for regs, wr in ((reads, False), (writes, True)):
+            for b, lo, hi in regs:
+                ps = psum(b)
+                for h in hist.get(b, ()):
+                    same = h[3] == q
+                    if same and q == "P":
+                        continue
+                    over = h[0] < hi and lo < h[1]
+                    if ((ps and not same) or (over and (h[2] or wr))) and want.get(h[3], 0) < h[4]:
+                        want[h[3]] = h[4]
+        for e, c in sorted(want.items(), key=lambda x: (x[0] == q, x[0])):
+            k = know[q]
+            if k.get(e, 0) < c:
+                eng[q].wait_ge(T.sem["s" + e if e in cnt else e], c)
+                for e2, c2 in list(snap.get((e, c), {}).items()) + [(e, c)]:
+                    if k.get(e2, 0) < c2:
+                        k[e2] = c2
+
+    def log(reads, writes, e, c):
+        for regs, wr in ((reads, False), (writes, True)):
+            for b, lo, hi in regs:
+                h = hist.setdefault(b, [])
+                h[:] = [x for x in h if not (lo <= x[0] and x[1] <= hi and
+                                             ((x[3] == e and x[2] == wr) or (wr and not psum(b))))]
+                h.append([lo, hi, wr, e, c])
+
+    def add(q, calls, rd, wr, dur, lat=0.0, sem=None, val=16, dep=()):
+        nodes.append({"q": q, "calls": calls, "rd": rd, "wr": wr, "dur": dur, "lat": lat, "sem": sem, "val": val, "dep": tuple(dep), "key": key[0]})
+        key[0] += 1
+        return len(nodes) - 1
+
+    def emit():
+        if "order" not in ORDERS:
+            ORDERS["order"] = plan(nodes)
+        for i in ORDERS["order"]:
+            x = nodes[i]
+            q, sem = x["q"], x["sem"]
+            if q == "R":
+                log([], x["wr"], sem, x["val"])
+                continue
+            wait(q, x["rd"], x["wr"])
+            for j, call in enumerate(x["calls"]):
+                ins = call()
+                if sem is None and j == len(x["calls"]) - 1:
+                    ins.then_inc(T.sem["s" + q], 1)
+                    cnt[q] += 1
+                    snap[(q, cnt[q])] = dict(know[q])
+                    log(x["rd"], x["wr"], q, cnt[q])
+                elif sem is not None and sem[0] == "d":
+                    ins.then_inc(T.sem[sem], 16)
+                    snap[(sem, 16)] = dict(know[q])
+                    log(x["rd"], x["wr"], sem, 16)
+
+    def count(k):
+        old, key[0] = key[0], k
+        return old
+
+    return add, emit, cnt, count
+
+
+def rank_program(g, core, T, topo):
+    rank = T.rank_of(core)
+    if rank is None:
+        return
+    add, emit, cnt, count = builder(g, T)
+    V = g.vector
+
+    def op(q, call, rd, wr, cycles, plus=0.0):
+        add(q, [call], rd, wr, plus + max(64, cycles) * CYC)
+
+    def dma(q, sem, out, in_, rd, wr, us=3.5):
+        add(q, [lambda: (g.sync if q == "Y" else g.scalar).dma_start(out=out, in_=in_)], rd, wr, 0.1, us, sem)
+
+    def size(r):
+        r = reg(r)
+        return r[2] - r[1]
+
+    def inds(*xs):
+        return any(isinstance(x, tuple) and len(x) == 2 for x in xs)
+
+    def small(*xs):
+        return all(reg(x)[0] in TWO for x in xs)
+
+    def v(r):
+        r = reg(r)
+        b, o = PLACE.get(r[0], (r[0], 0))
+        return T[b][:, o + r[1]:o + r[2]]
+
+    def back(b):
+        n, (b, o) = COLS[b], PLACE.get(b, (b, 0))
+        return T[b][:, o + n - 1:(o - 1 if o else None):-1]
+
+    def src(x, rd):
+        if isinstance(x, tuple) and len(x) == 2:
+            a, b = reg(x[0]), reg(x[1])
+            rd += [a, b]
+            return v(a).indirect(v(b))
+        if isinstance(x, (tuple, str)):
+            rd.append(reg(x))
+            return v(x)
+        return x
+
+    def tt(o, a, b, f):
+        rd = []
+        x, y = src(a, rd), src(b, rd)
+        op("V", lambda: V.tensor_tensor(out=v(o), in0=x, in1=y, op=f), rd, [reg(o)],
+           size(o) * (GATHER if inds(a, b) else 1 if any(psum(r[0]) for r in rd + [reg(o)]) else 2), 0.06 * inds(a, b))
+
+    def ts(o, a, s1, f0, s2=None, f1=None):
+        rd = []
+        x, y, z = src(a, rd), src(s1, rd), src(s2, rd)
+        c = size(o) * (GATHER if inds(a) else 0.5 if small(o, a) else 1)
+        if f1 is None:
+            op("V", lambda: V.tensor_scalar(out=v(o), in0=x, scalar1=y, scalar2=None, op0=f0), rd, [reg(o)], c)
+        else:
+            op("V", lambda: V.tensor_scalar(out=v(o), in0=x, scalar1=y, scalar2=z, op0=f0, op1=f1), rd, [reg(o)], c)
+
+    def cp(o, a):
+        rd = []
+        x = src(a, rd)
+        op("V", lambda: V.tensor_copy(out=v(o), in_=x), rd, [reg(o)], size(o) * (GATHER if inds(a) else 0.5 if small(o, a) else 1))
+
+    def scatter(win, lst, a):
+        op("V", lambda: V.tensor_copy(out=v(win).indirect(v(lst)), in_=v(a)), [reg(a), reg(lst)], [win], 3.8 * size(a))
+
+    def tr(o, a, f):
+        op("V", lambda: V.tensor_reduce(out=v(o), in_=v(a), axis=AxisListType.X, op=f), [reg(a)], [reg(o)], size(a))
+
+    def scan(o, a, b, ini, f0, f1, turn=False):
+        w = back if turn else v
+        op("V", lambda: V.tensor_tensor_scan(out=w(o), data0=w(a), data1=w(b), initial=ini, op0=f0, op1=f1), [reg(a), reg(b)], [reg(o)], size(o))
+
+    def act(o, a, fn, scale=1.0, bias=0.0, acc=None):
+        rd, wr = [], [reg(o)]
+        x, s, b = src(a, rd), src(scale, rd), src(bias, rd)
+        if acc is None:
+            op("S", lambda: g.scalar.activation(out=v(o), in_=x, func=fn, bias=b, scale=s), rd, wr, size(o) * (GATHER if inds(a) else 1), 0.03)
+        else:
+            op("S", lambda: g.scalar.activation(out=v(o), in_=x, func=fn, bias=b, scale=s, accum_out=v(acc)), rd, wr + [reg(acc)], size(o), 0.05)
+
+    def mms(o, *pairs, start=True, stop=True, dep=()):
+        def one(j, l, r):
+            rap = T[r[0]][:, r[1] + r[3]:r[2]:r[4]] if len(r) == 5 else v(r)
+            return lambda: g.tensor.matmul(out=v(o), lhsT=v(l), rhs=rap, start=start and j == 0, stop=stop and j == len(pairs) - 1)
+        pairs = [(reg(l), reg(r)) for l, r in pairs]
+        four = 1 if pairs[0][1][0] in TWO else 4
+        return add("P", [one(j, l, r) for j, (l, r) in enumerate(pairs)], [p for l, r in pairs for p in (l, r[:3])], [reg(o)],
+                   max(64, size(o)) * four * len(pairs) * 0.5e-3, dep=dep)
+
+    def iota(o, pattern, base, cm, small=False):
+        if small:
+            op("G", lambda: g.iota(v(o), pattern, base, cm, allow_small_or_imprecise_dtypes=True), [], [reg(o)], 2 * size(o), 0.13)
+        else:
+            op("G", lambda: g.iota(v(o), pattern, base, cm), [], [reg(o)], 2 * size(o), 0.13)
+
+    def zero(o):
+        iota(o, [[0, size(o)]], 0, 0, reg(o)[0] not in ("UW", "FW", "KW"))
+
+    def rowsum(b, r, i, base=0):
+        return ((b, base + 15 - i, base + 143 - i), r + (i, 16))
+
+    def POOL(t, lo, hi):
+        return ("POOL", t * POOLW + lo, t * POOLW + hi)
+
+    AND, SHR, ADD, SUB, MUL, MIN, MAX = Op.bitwise_and, Op.logical_shift_right, Op.add, Op.subtract, Op.mult, Op.min, Op.max
+    EQ, NE, GE, GT, LT, LE = Op.is_equal, Op.not_equal, Op.is_ge, Op.is_gt, Op.is_lt, Op.is_le
+
+    mate, far = T.cores[rank ^ 1], T.cores[rank ^ 4]
+    fe = topo.engines(core, far)
+    me = [e for e in topo.engines(core, mate) if e not in fe][:len(fe)]
+    half = len(fe) // 2
+
+    def transfer(dst, es, sem, a, b):
+        rid, pid = topo.addr(dst, core)
+        return RemoteDMATransfer(dst_ids=[DstId(rid=rid, pnc=pid)], dma_engine_mask=sum(1 << e for e in es), remote_sem=T.sem[sem], src=v(a), dst=v(b))
+    sent = len(fe) + len(me)
+
+    def send(sem, transfers, a, land):
+        i = add("G", [lambda: g.remote_dma_fused(transfers, local_sem=T.sem.lsem)], [a], [], 1.0, sem="rem")
+        add("R", [], [], [land], 0.0, 2.2, sem, sent, (i,))
+
+    count(-1000)
+    for q, sem, b, x in (("Y", "dG", "GL", T.gd[:, :]), ("S", "dW", "wi", T.wt[:, :]), ("Y", "dX", "X:0:2048", T.xs[:, 0:2048]),
+                         ("S", "dX2", "X:2048:4096", T.xs[:, 2048:4096]), ("S", "dK", "ki", T.km[:, :]), ("S", "dT", "ti", T.th[:, :]),
+                         ("Y", "dR", "R0", T.xs[0:128:16, :])):
+        dma(q, sem, v(b), x, [], [reg(b)])
+
+    iota("IP", [[0, 1]], 0, 1)
+    iota("IZ", [[1, 144]], -15, 0)
+    iota("IQ", [[1, 144]], 0, 0)
+    iota("IJ", [[16, 80]], 0, 0)
+    iota("R48", [[1, 48]], 2049, 0, True)
+    iota("RI", [[1, 48]], 0, 0, True)
+    iota("I256", [[1, 256]], 0, 0)
+    iota("IO", [[1, 256]], 0, 0, True)
+    iota("C2", [[2, 12], [0, 64]], 0, 0, True)
+    for b in ("UW:64:80", "FW:64:80", "KW:64:80", "Q:64:80", "ZER", "CB"):
+        zero(b)
+    for k in range(3):
+        iota(R("YB", k, k + 1), [[0, 1]], (-7000, -16000, -32000)[k], 0, True)
+    for t in range(RO):
+        zero(R("SND", 384 * t, 384 * t + 192))
+        zero(POOL(t, 192 + S, POOLW))
+    IQ = "IQ:0:128"
+    ts("IPa", "IP", 15, AND)
+    ts("IPb", "IP", 4, SHR)
+    cp("Pf", "IP")
+    cp("PG", "IPb")
+    cp("PI", "IPa")
+    ts("P16", "PG", 16.0, MUL)
+    ts("IQa", IQ, 4, SHR)
+    ts("Z1", "IZ", "P16", EQ)
+    ts("B", "IQa", "PG", EQ)
+    cp("wf", "wi")
+    cp("wb", "wi")
+    mms("P3:0:3", ("B", "wb"))
+    for t in range(RO):
+        ts(R("ZW", 144 * t, 144 * t + 144), "Z1", R("wf", t, t + 1), MUL)
+    ts(POOL(0, 192, 192 + S), "GL", -255.0, ADD)
+    ts("SW", "P3:0:3", 255.0, MUL)
+    cp("KF", "ki")
+    ts("TH", "ti", 64.0, MUL)
+
+    def prod(m):
+        b, o = ((6, 0), (7, 0), (1, 0), (1, 192))[m // 3]
+        return R("P%d" % b, o + 64 * (m % 3), o + 64 * (m % 3) + 64)
+
+    def ulist(t):
+        mms("P2:0:64", *[rowsum("ZW", POOL(t, 192, 192 + S), i, 144 * t) for i in range(16)])
+        ts("u0", "P2:0:64", R("SW", t, t + 1), ADD)
+        ts("UW:0:64", "u0", 4095, AND)
+        cp("uf", "UW:0:64")
+        tt("f0", "UW:0:64", "UW:0:64", MUL)
+        for m in range(M):
+            act(prod(m), "uf", Fn.Copy, scale=R("KF", m, m + 1))
+        ts("FW:0:64", "f0", 5, SHR)
+
+    def clist(j):
+        lo, hi = 192 * j, 192 * j + 192
+        for q in range(3):
+            tt(R("CI", lo + 64 * q, lo + 64 * q + 64), prod(3 * j + q), "FW:0:64", ADD)
+        ts(R("CM", lo, hi), R("CI", lo, hi), 4095, AND)
+        cp(R("CL", lo, hi), R("CM", lo, hi))
+        ts(R("BI", lo, hi), R("CL", lo, hi), 4000.0, GE)
+
+    def consts1():
+        ts("ID", IQ, "Pf", EQ)
+        act("Z64", "Z1", Fn.Copy, scale=64.0)
+        act("Z128", "Z1", Fn.Copy, scale=128.0)
+        act("ZN", "Z1", Fn.Copy, scale=-64.0)
+
+    def consts2():
+        act("BF", "B", Fn.Copy)
+        act("NB", "B", Fn.Copy, scale=-1.0)
+        act("NI", "ID", Fn.Copy, scale=-1.0)
+        act("Y3", "ID", Fn.Copy, scale=1.5)
+        act("Y1", "ID", Fn.Copy, scale=-0.5)
+        ts("tA", IQ, "Pf", GT, -1.0, MUL)
+        ts("tC", IQ, "Pf", LT, -1.0, MUL)
+        ts("IQb", IQ, 15, AND)
+        ts("WI", "IQ:0:96", 15, AND)
+        act("tB", "ID", Fn.Copy, scale=1024.0)
+        tt("TN", "tA", "B", MUL)
+        tt("tC", "tC", "B", MUL)
+        ts("tA", "IQa", 16.0, MUL)
+        tt("TS", "tB", "TN", ADD)
+        act("tD", "ID", Fn.Copy, scale=2048.0)
+        ts("B0", "tA", "Pf", EQ, 4.0, MUL)
+        tt("TQ", "tD", "tC", ADD)
+        act("tE", "TN", Fn.Copy, scale=2.0)
+        ts("tA", "IQb", 1000.0, ADD)
+        tt("TG", "tE", "NI", ADD)
+        ts("WM", "WI", "PI", EQ)
+        tt("tC", "tA", "B", MUL)
+        ts("SLW", "IJ", "PI", ADD)
+        ts("AG", "tC", -1000.0, ADD)
+        ts("tA", "IQb", -1000.0, ADD)
+        act("IO16", "IO:0:64", Fn.Copy, scale=16.0)
+        tt("tA", "tA", "B", MUL)
+        ts("AGp", "tA", 1000.0, ADD)
+        ts("P256", "PI", 256.0, MUL)
+        ts("RBH", "SLW:0:3", 0.5, ADD)
+        ts("RC", "SLW:0:3", -1.0, MUL, 832.0, ADD)
+        ts("PL", "I256", "P256", ADD)
+        ts("BM", "I256:0:16", "PI", LE, 16384.0, MUL)
+        ts("EG:0", "PI", 3.0, GE, 5000.0, MUL)
+        ts("EG:1", "PI", 0.0, EQ, -1.0, MUL)
+        ts("EG:2", "PI", 1.0, GE, -1.0, MUL)
+        tt("junk:0:12", "WM:0:12", "KF", MUL)
+        tr("KD", "junk:0:12", ADD)
+
+    def utable():
+        ts("NK", "R0", 192.0, LT)
+        scan("TU", "NK", "PL", 32768.0, MUL, MAX, True)
+        ts("fw", "WM:0:16", "TU:0", MUL)
+        mms("P7:0:16", ("BF", "fw"))
+        tt("junk:16:32", "P7:0:16", "BM", ADD)
+        tr("nf", "junk:16:32", MIN)
+        ts("UT", "TU", "nf", MIN, 4095.0, MIN)
+
+    def three(f, o, w, a):
+        o, a = reg(o), reg(a)
+        for k in range(3):
+            f(sub(o, k, k + 1), sub(a, w * k, w * k + w))
+
+    def vsum(o, a):
+        tr(o, a, ADD)
+
+    def ssum(o, a):
+        act(R("junk", 64 * (o[1] % 3), 64 * (o[1] % 3) + 16), a, Fn.Copy, acc=o)
+
+    for t in range(RO):
+        own = POOL(t, 192, 192 + S)
+        count(0)
+        ulist(t)
+        if t == 0:
+            k = count(-1000)
+            consts1()
+            count(k)
+        for j in range(4):
+            clist(j)
+        parts = {}
+        for b, m, n in ((0, 0, 6), (1, 6, 3), (6, 9, 3)):
+            parts[b] = [mms(R("P%d" % b, 0, 64 * n), *[("ID", R(x, 64 * m, 64 * (m + n))) for x in ("C2", "BI")], stop=False)]
+        for m in range(M):
+            Zm, Am, Cl = R("Z", S * m, S * m + S), R("A", S * m, S * m + S), R("CL", 64 * m, 64 * m + 64)
+            if m in SMS:
+                act(Zm, ("X", Cl), Fn.Copy)
+                for h in range(2):
+                    o, lo = "P%d" % (2 + h + 2 * (SMS.index(m) % 2)), 512 * h
+                    mms(o, ("ID", sub(own, lo, lo + 512)), ("ID", sub(Zm, lo, lo + 512)))
+                    act(sub(Am, lo, lo + 512), o, Fn.Abs)
+            else:
+                tt(Zm, ("X", Cl), own, ADD)
+                if m in RMS:
+                    ts(Am, Zm, 0.0, MAX)
+                else:
+                    act(Am, Zm, Fn.Abs)
+            b, n, last = (0, m, m == 5) if m < 6 else (1, m - 6, m == 8) if m < 9 else (6, m - 9, m == 11)
+            for z, x in (("ZN", Zm), ("Z128", Am)) if m in RMS else (("Z64", Am),):
+                stop = last and x is Am
+                parts[b].append(mms(R("P%d" % b, 64 * n, 64 * n + 64), *[rowsum(z, x, i) for i in range(16)],
+                                    start=False, stop=stop, dep=parts[b] if stop else ()))
+        if t == 0:
+            k = count(-1000)
+            consts2()
+            utable()
+            count(k)
+        cp("cur", "P0:0:192")
+        tt("cur", "cur", "P0:192:384", MIN)
+        tt("cur", "cur", "P1:0:192", MIN)
+        tt("cur", "cur", "P6:0:192", MIN)
+        tt("fa", "cur:0:64", "cur:64:128", MIN)
+        tt("KW:0:64", "fa", "cur:128:192", MIN)
+        ts("fb", "KW:0:64", 1, AND)
+        ts("fa", "KW:0:64", "TH", LT)
+        tt("FB", "fa", "fb", GT)
+        mms("P2:0:64", ("B", "FB"))
+        mms("P3:0:64", ("TQ", "FB"))
+        scan("Cs", "P2:0:64", "ZER", 0.0, ADD, ADD)
+        for k in range(3):
+            act(R("junk", 64 * k, 64 * k + 64), "Cs", Fn.Sign, scale=-1.0, bias=R("RBH", k, k + 1), acc=R("sA", k, k + 1))
+        tt("Q:0:64", "Cs", "P3:0:64", ADD)
+        ts("RV", "RI", "Cs:63", GE, 1048576.0, MUL)
+        ts("vl", "SLW:0:3", "Cs:63", LT)
+        tt("RV", "RV", "RI", ADD)
+        so = "sO:0:3"
+        ts(so, "sA", 0.5, MUL, 32.0, ADD)
+        tt("OH", ("Q", so), "R48", EQ)
+        tt("M1:0:48", ("KW", so), "OH", MUL)
+        mms("P4:0:48", ("BF", "M1:0:48"))
+        for j, b in enumerate(("UW", "FW", "SLW")):
+            tt(R("M1", 48 * j + 48, 48 * j + 96), (b, so), "OH", MUL)
+        mms("P5:0:144", ("BF", "M1:48:192"))
+        act("US", "P5:0:144", Fn.Copy)
+        cp("kI", "P4:0:48")
+        ts("mI", "kI", 1, SHR, 15, AND)
+        ts("dm", "kI", 0x7FFFC0, AND)
+        ts("xk", "mI", "PI", EQ, "KD", MUL)
+        mms("P6:0:48", ("BF", "xk"))
+        tt("CK:48:96", "dm", "RV", ADD)
+        tt("tk", "P6:0:48", "US:0:48", MUL)
+        tt("ts", "tk", "US:48:96", ADD)
+        ts("CK:0:48", "ts", 4095, AND)
+        tt("CKm", "CK", "WM", MUL)
+        three(ssum, "kw", 16, "CKm:48:96")
+        three(vsum, "cw", 16, "CKm:0:48")
+        ts("p1", "CK:0:48", 16.0, ADD)
+        ts("q1", "cw", 16.0, ADD)
+        ts("p1h", "p1", 8, SHR)
+        ts("q1l", "q1", 255, AND)
+        ts("sel", "p1h", "PI", EQ)
+        cp("qO:0:3", "q1l")
+        tt("T1", ("UT", "qO:0:3"), "sel", MUL)
+        mms("P7:0:48", ("BF", "T1"))
+        for k in range(3):
+            ts(R("tm", 48 * k, 48 * k + 48), "CK:0:48", R("cw", k, k + 1), NE, 2097152.0, MUL)
+        for k in range(3):
+            tt(R("tm", 48 * k, 48 * k + 48), R("tm", 48 * k, 48 * k + 48), "CK:48:96", ADD)
+        tt("em", "P7:0:48", "WM:0:48", MUL)
+        ts("p1", "P7:0:48", 8.0, ADD, 4095.0, MIN)
+        three(vsum, "ew:0:3", 16, "em")
+        ts("p1h", "p1", 8, SHR)
+        ts("q1", "ew:0:3", 8.0, ADD, 4095.0, MIN)
+        ts("sel", "p1h", "PI", EQ)
+        ts("q1l", "q1", 255, AND)
+        cp("qO:0:3", "q1l")
+        tt("T1", ("UT", "qO:0:3"), "sel", MUL)
+        mms("P7:0:48", ("BF", "T1"))
+        three(lambda o, a: tr(o, a, MIN), "mn", 48, "tm")
+        tt("eq", "mn", "kw", EQ)
+        tt("CB:2:5", "eq", "vl", MUL)
+        mms("P3:0:1", ("B", "CB:2"), ("B", "CB:3"), ("B", "CB:4"))
+        mms("P2:0:3", ("TS", "CB:2:5"), ("NB", "CB:1:4"), ("NB", "CB:0:3"))
+        ts("OFF:0:3", "cw", 10.0, ADD)
+        cp("OFF:3:6", "ew:0:3")
+        tt("em", "P7:0:48", "WM:0:48", MUL)
+        three(vsum, "ew:3:6", 16, "em")
+        cn = R("CN", t, t + 1)
+        cp(cn, "P3:0:1")
+        cp("OFF:6:9", "ew:3:6")
+        send("cn%d" % t, [transfer(far, fe, "cn%d" % t, cn, R("CNL", 2 * t + 1, 2 * t + 2)),
+                          transfer(mate, me, "cn%d" % t, cn, R("CNL", 2 * t, 2 * t + 1))], cn, R("CNL", 2 * t, 2 * t + 2))
+        cp("GX", ("X", "OFF:0:9"))
+        ts("GN", "GX", 0.0, MIN)
+        mms("P5:0:144", ("NI", "GX"), ("B0", "GN"))
+        tt("vv", "P2:0:3", "RC", MAX)
+        for b in range(3):
+            ts(R("DL", 3 * b, 3 * b + 3), "vv", -1.0, MUL, 1024.0 + 64 * b, ADD)
+        tt("SLm", "US:96:144", "WM:0:48", MUL)
+        ts("GV", "P5:0:144", -255.0, MAX)
+        snd = R("SND", 384 * t, 384 * t + 384)
+        scatter(snd, "DL:0:9", "GV")
+        send("ar%d" % t, [transfer(far, fe[:half], "ar%d" % t, sub(snd, 64, 128), POOL(t, 64, 128)),
+                          transfer(far, fe[half:], "ar%d" % t, sub(snd, 128, 192), POOL(t, 128, 192)),
+                          transfer(mate, me, "ar%d" % t, sub(snd, 0, 64), POOL(t, 0, 64))], snd, POOL(t, 0, 192))
+        three(ssum, "sw", 16, "SLm")
+        ts("nc", "CB:2:5", -100.0, MUL, 100.0, ADD)
+        cp("CE:0:3", "cw")
+        ts("CE:3:6", "ew:3:6", 1.0, ADD)
+        ts("CE:12:18", "CE:0:6", 255, AND)
+        ts("CE:6:12", "CE:0:6", 8, SHR)
+        ts("CF:6:9", "CE:12:15", -1.0, MUL, 0.5, ADD)
+        ts("CF:9:12", "CE:15:18", 0.5, SUB)
+        tt("CF:0:3", "CE:6:9", "nc", ADD)
+        tt("CF:3:6", "CE:9:12", "nc", ADD)
+        LHk = [R("LH", 128 * k, 128 * k + 128) for k in range(8)]
+        RHk = [R("RH", 256 * k, 256 * k + 256) for k in range(6)]
+        for k in range(6):
+            act(RHk[k], "IO", Fn.Sign, scale=1.0 if k < 3 else -1.0, bias=R("CF", 6 + k, 7 + k))
+            ts(LHk[k], "AG", R("CF", k, k + 1), EQ)
+        mms("P7:0:256", *zip(LHk, RHk))
+        cp("sl16:0:3", "sw")
+        cp("tg", (own, "sl16:0:3"))
+        scatter(POOL(t, 192 + S, POOLW), "DL:0:3", "tg")
+        ts("n5", "CB:2:5", -5000.0, MUL, 5000.0, ADD)
+        tt("pv", "sw", "vv", ADD)
+        tt("pv", "pv", "n5", ADD)
+        cp("lc", "P7:255")
+        mms("P3:0:1", ("TG", "lc"))
+        ts("P7:0:256", "P7:0:256", "P3:0:1", GT, -32768.0 / 2 ** t, MUL)
+        tt("R0", "R0", "P7:0:256", ADD)
+        if t < RO - 1:
+            dma("Y", "dM%d" % t, T.X[0:128:16, :], T.R0[:], [R("R0")], [R("X")])
+        n1, n2 = R("CNL", 2 * t, 2 * t + 1), R("CNL", 2 * t + 1, 2 * t + 2)
+        ts("ac:0", n2, 2.0, MUL, n1, ADD)
+        ts("ac:2", n2, "PI", MUL, "EG:0", ADD)
+        ts("ac:1", n1, "EG:1", MUL, 64.0, ADD)
+        ts("PO:0:3", "pv", "ac:0", ADD, -1024.0, ADD)
+        ts("PJ:0:3", "pv", "ac:0", ADD, -1024.0, ADD)
+        ts("PJ:3", "ac:2", n1, ADD)
+        ts("PO:3", "ac:2", n1, ADD)
+        ts("wt4", n2, "EG:2", MUL, "ac:1", ADD)
+        ts("PJ:4:8", "PJ:0:4", 15, AND)
+        cp("PF", "PJ:4:8")
+        pairs = []
+        for k in range(4):
+            a, b, pos, lo = sub(RHk[k], 0, 64), sub(RHk[k], 64, 128), R("PO", k, k + 1), R("PF", k, k + 1)
+            w = ("wt4", MUL) if k == 3 else ()
+            ts(a, "IO16", 15.0, ADD, pos, GE)
+            ts(b, "IO16", pos, GT)
+            ts(LHk[k], "AG", lo, GE, *w)
+            ts(LHk[4 + k], "AGp", lo, LT, *w)
+            pairs += [(LHk[k], a), (LHk[4 + k], b)]
+        mms("P6:0:64", *pairs)
+        tt("lf", "P6:0:64", "SLW:0:64", ADD)
+        cp("LST", "lf")
+        pool = POOL(t, 0, POOLW)
+        if t < RO - 1:
+            utable()
+            nxt = POOL(t + 1, 192, 192 + S)
+            cp(sub(nxt, 0, 512), (pool, "LST:0:32"))
+            act(sub(nxt, 512, 1024), (pool, "LST:32:64"), Fn.Copy)
+        else:
+            for k in range(3):
+                act(RHk[k], "R0", Fn.Sign, scale=-1.0, bias=R("YB", k, k + 1))
+            mms("P5:0:256", ("Y3", RHk[0]), ("Y1", RHk[1]), ("Y1", RHk[2]))
+            act("yct", "P5:0:256", Fn.Copy, bias=0.5)
+            dma("Y", "dC", T.yc[:, :], v("yct"), [R("yct")], [])
+            ts("YG:0:512", (pool, "LST:0:32"), 255.0, ADD)
+            act("YG:512:1024", (pool, "LST:32:64"), Fn.Copy, bias=255.0)
+            dma("Y", "dY0", T.yg[:, 0:512], T.YG[:, 0:512], [R("YG", 0, 512)], [])
+            dma("S", "dY1", T.yg[:, 512:1024], T.YG[:, 512:1024], [R("YG", 512, 1024)], [])
+    emit()
+    g.wait_ge(T.sem.lsem, 2 * RO * sent)
+    for e, n in list(cnt.items()) + [(d, 16) for d in LOADS]:
+        g.wait_ge(T.sem["s" + e if e in cnt else e], n)

@@ -2,17 +2,19 @@ from concourse.bass import DstId, RemoteDMATransfer
 from concourse.mybir import AluOpType as Op, AxisListType, ActivationFunctionType as Fn
 
 RO, M, S, W, CAP = 3, 12, 1024, 4096, 48
-POOLW = 192 + S + 240
-_F32 = """wf 3 KF 12 TH 1 KD 1 SW 3 Pf 1 PI 1 PG 1 P16 1 P256 1 BF 128 tA 128 tB 128 tC 128 tD 128 tE 128 WM 96 R48 48 RI 48 SLW 80 RBH 3 RC 3
- PL 256 BM 16 EG 4 ZER 64 uf 64 Q 80 cur 192 fa 64 Cs 64 junk 192 sA 3 OH 48 M1 192 xk 48 US 144 tk 48 RV 48 vl 3 CKm 96 SLm 48 cw 3 kw 3 sw 3
- tm 144 mn 3 eq 3 vv 3 nc 3 n5 3 pv 3 sel 48 T1 48 em 48 ew 6 UT 256 TU 256 fw 16 nf 1 wt4 1 CF 12 PO 4 ac 3 PF 4 lf 64
- yct 256 YB 3 CN 3 CNL 6"""
-_BF = """X 4096 GL 1024 YG 1024 Z 12288 A 12288 wb 3 Z1 144 Z64 144 Z128 144 ZN 144 ZW 432 B 128 NB 128 ID 128 NI 128 TN 128 TS 128 TQ 128
- B0 128 TG 128 Y3 128 Y1 128 AG 128 AGp 128 IO16 64 IO 256 BI 768 C2 768 FB 64 CB 8 GX 144 GN 144 GV 144 LH 1024 RH 1536 lc 1 R0 256 NK 256
- tg 48 SND 1152 POOL 4368"""
-_I32 = """wi 3 ki 12 ti 1 IP 1 IPa 1 IPb 1 IQ 144 IQa 128 IQb 128 IZ 144 IJ 80 I256 256 WI 96 UW 80 FW 80 KW 80 u0 64 f0 64 CI 768 CM 768
- fb 64 kI 48 mI 48 dm 48 ts 48 CK 96 p1 48 p1h 48 q1 3 q1l 3 CE 18 PJ 8"""
-_U16 = "CL 768 sO 4 DL 12 OFF 12 qO 4 LST 64 sl16 4"
+OWNW, ARPW, SNDW = S + 192, 144 + S, 288
+E2 = 272
+_F32 = """wf 3 wn 3 KF 16 TH 1 SW 3 Pf 1 PI 1 PG 1 P16 1 P256 1 H15 1 K2 2 BF 128 BK 128 IDF 128 IDB 128 SHF 128 tA 128 tB 128 tC 128 tD 128
+ WM 96 R48 48 SLW 80 SL6 6 SL24 64 IA 64 IB 64 RBH 3 RC 3 PL 256 BM 16 ZER 64 uf 64 Q 80 TM 128 cur 64 Cs 64 junk 192 jk2 192 sA 3 IV 6
+ M1 144 CKk 48 KM 48 kw 3 WS 3 ncw 3 sel 96 T2 96 em 96 ew 6 TK 144 lose 3 vv 3 swn 3 npos 3 PF 3 s1 9 CFl 6 CFh 6
+ UE 528 TU 256 TE 256 fw 16 fw2 16 nf 1 nf2 1 yct 256 CN 12 CNL 24"""
+_BF = """X 4096 GL 1024 YG 1024 Z 12288 A 12288 wb 3 Z1 144 Z64 144 ZN 144 ZP 144 ZW 432 GI 8 GN8 8 B 128 NB 128 B2N 128 ID 128 NI 128 ID16 128
+ ID8 128 TN 128 TS 128 TS2 128 TQ 128 B0 128 Y3 128 Y1 128 AG 128 AGp 128 AG8 128 IO 256 ONP 256 ONN 256 RI 48 SLb 16 BI 768 C2 768 FB 64
+ OH 48 Mm 48 RVi 48 sob 3 HL 96 CB 8 GX 144 GN 144 GV 144 LH 768 LG 768 RH 1536 LL 768 SS 384 HT 48 R0 256 NK 256 FY 768 tg 48
+ SND 864 OWN 3648 ARP 3504"""
+_I32 = """wi 3 ki 12 ti 1 IP 1 IPa 1 IPb 1 IQ 144 IQa 128 IQb 128 IZ 144 IJ 80 I256 256 WI 96 UW 80 FW 80 KW 80 MW 80 u0 64 f0 64 CI 768 CM 768
+ fb 64 xi 48 xh 48 xl 48 CE 18 pos 3 posl 3"""
+_U16 = "CL 768 sO 4 DL 12 OFF 12 qO 8 LR 64 L2 66 sl16 4 LPI 8"
 COLS, SCRATCH, PLACE = {}, {}, {}
 for _txt, _dt in ((_F32, "float32"), (_BF, "bfloat16"), (_I32, "int32"), (_U16, "uint16")):
     _w, _at = _txt.split(), 16
@@ -29,11 +31,12 @@ for _txt, _dt in ((_F32, "float32"), (_BF, "bfloat16"), (_I32, "int32"), (_U16, 
 for _b in range(8):
     SCRATCH["P%d" % _b] = ("psum", [128, 512], "float32")
     COLS["P%d" % _b] = 512
-LOADS = ["dG", "dW", "dK", "dT", "dX", "dX2", "dR", "dM0", "dM1", "dY0", "dY1", "dC"]
+LOADS = ["dG", "dW", "dK", "dT", "dX", "dX2", "dR", "dM0", "dM1", "dY0", "dY1", "dY2", "dC"]
 SEMAPHORES = ["sV", "sS", "sP", "sG", "lsem", "cn0", "cn1", "cn2", "ar0", "ar1", "ar2"] + LOADS
 
-SMS = (0, 1, 3, 6)
-RMS = (9, 10, 11)
+KIND = "SSVVSSVVVVSS"
+PAIRS = 5
+CHUNKS = ((0, 1), (1, 3), (3, 7), (7, 12))
 
 
 def R(b, lo=0, hi=None):
@@ -49,12 +52,16 @@ def reg(x):
 
 
 def sub(r, lo, hi):
+    r = reg(r)
     return (r[0], r[1] + lo, r[1] + hi)
 
 
-WAKE, CYC, GATHER, SLACK = 0.12, 1.04e-3, 1.5, 0.10
-HINT = ("04063769656271386045144780815589920545733890020253425010900001080800440909354774405107808900080800275990981087050920792303210856000859"
-        "020324062016193719011460005540009729252008968738078207900107450755950678724219169209800513049000919002101803720839245550202005003002061")
+def col(r, k):
+    return sub(r, k, k + 1)
+
+
+WAKE, CYC, GATHER, PE, SLACK = 0.15, 1.04e-3, 1.56, 0.55e-3, 0.1
+PASSES, STEPS, EASE = 4, 20000, 0.3
 TWO = {_k for _t in (_BF, _U16) for _k in _t.split()}
 ORDERS = {}
 
@@ -63,57 +70,133 @@ def psum(b):
     return b[0] == "P" and b[1:] in "01234567" and len(b) == 2
 
 
-def plan(nodes):
-    n, hist = len(nodes), {}
-    pre, suc = [set() for _ in nodes], [[] for _ in nodes]
+def links(nodes):
+    hist, pre, bank = {}, [set() for _ in nodes], {}
     for i, x in enumerate(nodes):
         for regs, wr in ((x["rd"], False), (x["wr"], True)):
             for b, lo, hi in regs:
-                for l, h, w, j, q in hist.get(b, ()):
-                    if (l < hi and lo < h and (w or wr)) or (psum(b) and q != x["q"]):
+                for l, h, w, j in hist.get(b, ()):
+                    if l < hi and lo < h and (w or wr):
                         pre[i].add(j)
         pre[i].update(x["dep"])
+        if x["q"] == "P":
+            group, since = bank.setdefault(x["wr"][0][0], ([], []))
+            pre[i].update(group + since if x["grp"] else group)
+            if x["grp"]:
+                group[:], since[:] = [i], []
+            else:
+                since.append(i)
         pre[i].discard(i)
         for regs, wr in ((x["rd"], False), (x["wr"], True)):
             for b, lo, hi in regs:
                 h = hist.setdefault(b, [])
-                if wr and not psum(b):
+                if wr:
                     h[:] = [e for e in h if not (lo <= e[0] and e[1] <= hi)]
-                h.append((lo, hi, wr, i, x["q"]))
-        for j in pre[i]:
-            suc[j].append(i)
-    prio = [0.0] * n
-    for i in range(n - 1, -1, -1):
-        prio[i] = nodes[i]["dur"] + nodes[i]["lat"] + max([prio[j] + WAKE for j in suc[i]], default=0.0)
-    prio = [p + 0.5 * int(HINT[x["key"]]) if 0 <= x["key"] < len(HINT) else p for p, x in zip(prio, nodes)]
-    left, rdy = [len(p) for p in pre], [0.0] * n
-    ready, free, order = {}, {}, []
+                h.append((lo, hi, wr, i))
+    return pre
+
+
+def lay(nodes, pre, suc, prio):
+    n = len(nodes)
+    left, rdy, end, ready, free, order = [len(p) for p in pre], [0.0] * n, [0.0] * n, {}, {}, []
     for i in range(n):
         if not left[i]:
             ready.setdefault(nodes[i]["q"], []).append(i)
     while len(order) < n:
         best = None
         for q, l in ready.items():
-            if not l:
-                continue
-            f = free.get(q, 0.0)
-            t = min(max(f, rdy[i]) for i in l) + SLACK
-            i = max((i for i in l if max(f, rdy[i]) <= t), key=lambda i: (prio[i], -i))
-            s = max(f, rdy[i])
-            if best is None or s < best[0]:
-                best = (s, q, i)
+            if l:
+                f = free.get(q, 0.0)
+                t = max(f, min(rdy[i] for i in l)) + SLACK
+                i = max((i for i in l if rdy[i] <= t), key=lambda i: (prio[i], -i))
+                if best is None or max(f, rdy[i]) < best[0]:
+                    best = (max(f, rdy[i]), q, i)
         s, q, i = best
         ready[q].remove(i)
         order.append(i)
         if q != "R":
             free[q] = s + nodes[i]["dur"]
-        end = s + nodes[i]["dur"] + nodes[i]["lat"] + WAKE
+        end[i] = s + nodes[i]["dur"] + nodes[i]["lat"]
         for j in suc[i]:
-            rdy[j] = max(rdy[j], end)
+            rdy[j] = max(rdy[j], end[i] + WAKE)
             left[j] -= 1
             if not left[j]:
                 ready.setdefault(nodes[j]["q"], []).append(j)
-    return order
+    return order, end
+
+
+def plan(nodes):
+    n, pre = len(nodes), links(nodes)
+    suc = [[] for _ in nodes]
+    for i in range(n):
+        for j in pre[i]:
+            suc[j].append(i)
+    qs, dur, lat = [x["q"] for x in nodes], [x["dur"] for x in nodes], [x["lat"] for x in nodes]
+    need = [[(j, 0.0 if qs[i] == qs[j] == "P" else WAKE) for j in pre[i]] for i in range(n)]
+    banks = [sorted({r[0] for r in x["rd"] + x["wr"] if psum(r[0])}) for x in nodes]
+
+    def run(order):
+        end, why, free, held = [0.0] * n, [None] * n, {}, {"P%d" % b: {} for b in range(8)}
+        for i in order:
+            s, w, q = 0.0, None, qs[i]
+            for j, d in need[i]:
+                if end[j] + d > s:
+                    s, w = end[j] + d, (j, True)
+            f = free.get(q)
+            if f is not None and end[f] - lat[f] > s:
+                s, w = end[f] - lat[f], (f, False)
+            for b in banks[i]:
+                for p, j in held[b].items():
+                    if p != q and end[j] + WAKE > s:
+                        s, w = end[j] + WAKE, (j, False)
+                held[b][q] = i
+            end[i], why[i] = s + dur[i] + lat[i], w
+            if q != "R":
+                free[q] = i
+        e = max(end)
+        return e, why, end.index(e), order
+
+    def swap(order, j, i, early):
+        a, b = order.index(j), order.index(i)
+        part, move = order[a:b + 1], {i if early else j}
+        for k in (reversed(part) if early else part):
+            if k in move:
+                move.update(pre[k] if early else suc[k])
+        if (j if early else i) in move:
+            return None
+        go, stay = [k for k in part if k in move], [k for k in part if k not in move]
+        return order[:a] + (go + stay if early else stay + go) + order[b + 1:]
+
+    prio = [0.0] * n
+    for i in range(n - 1, -1, -1):
+        prio[i] = dur[i] + lat[i] + max([prio[j] + WAKE for j in suc[i]], default=0.0)
+    tries = []
+    for _ in range(PASSES):
+        order, end = lay(nodes, pre, suc, prio)
+        tries.append(run(order))
+        prio = lay(nodes, suc, pre, end)[1]
+    cur = best = min(tries, key=lambda x: x[0])
+    seed = 1
+    for step in range(STEPS):
+        chain, i = [], cur[2]
+        while cur[1][i]:
+            chain.append((i, cur[1][i][1]))
+            i = cur[1][i][0]
+        chain.append((i, True))
+        spots = [k for k, x in enumerate(chain) if not x[1]]
+        seed = (seed * 1103515245 + 12345) % 2147483648
+        a = b = spots[(seed >> 8) % len(spots)]
+        for _ in range((seed >> 24) % 4):
+            b += not chain[b + 1][1]
+        new = swap(cur[3], chain[b + 1][0], chain[a][0], seed >> 29 & 1)
+        if new:
+            new = run(new)
+            if new[0] < cur[0] + EASE * (1 - step / STEPS) * ((seed >> 4) % 16) / 16:
+                cur = new
+                if cur[0] < best[0]:
+                    best = cur
+    ORDERS["end"] = best[:3] + (nodes,)
+    return best[3]
 
 
 def builder(g, T):
@@ -122,7 +205,7 @@ def builder(g, T):
     know = {q: {} for q in eng}
     snap = {}
     hist = {}
-    nodes, key = [], [0]
+    nodes = []
 
     def wait(q, reads, writes):
         want = {}
@@ -152,9 +235,8 @@ def builder(g, T):
                                              ((x[3] == e and x[2] == wr) or (wr and not psum(b))))]
                 h.append([lo, hi, wr, e, c])
 
-    def add(q, calls, rd, wr, dur, lat=0.0, sem=None, val=16, dep=()):
-        nodes.append({"q": q, "calls": calls, "rd": rd, "wr": wr, "dur": dur, "lat": lat, "sem": sem, "val": val, "dep": tuple(dep), "key": key[0]})
-        key[0] += 1
+    def add(q, calls, rd, wr, dur, lat=0.0, sem=None, val=16, dep=(), grp=False):
+        nodes.append({"q": q, "calls": calls, "rd": rd, "wr": wr, "dur": dur, "lat": lat, "sem": sem, "val": val, "dep": tuple(dep), "grp": grp})
         return len(nodes) - 1
 
     def emit():
@@ -179,29 +261,25 @@ def builder(g, T):
                     snap[(sem, 16)] = dict(know[q])
                     log(x["rd"], x["wr"], sem, 16)
 
-    def count(k):
-        old, key[0] = key[0], k
-        return old
-
-    return add, emit, cnt, count
+    return add, emit, cnt
 
 
 def rank_program(g, core, T, topo):
     rank = T.rank_of(core)
     if rank is None:
         return
-    add, emit, cnt, count = builder(g, T)
+    add, emit, cnt = builder(g, T)
     V = g.vector
 
     def op(q, call, rd, wr, cycles, plus=0.0):
         add(q, [call], rd, wr, plus + max(64, cycles) * CYC)
 
-    def dma(q, sem, out, in_, rd, wr, us=3.5):
+    def dma(q, sem, out, in_, rd, wr, us=2.5):
         add(q, [lambda: (g.sync if q == "Y" else g.scalar).dma_start(out=out, in_=in_)], rd, wr, 0.1, us, sem)
 
     def size(r):
         r = reg(r)
-        return r[2] - r[1]
+        return r[2] - r[1] if len(r) == 3 else (r[2] - r[1]) // r[4]
 
     def inds(*xs):
         return any(isinstance(x, tuple) and len(x) == 2 for x in xs)
@@ -212,11 +290,12 @@ def rank_program(g, core, T, topo):
     def v(r):
         r = reg(r)
         b, o = PLACE.get(r[0], (r[0], 0))
-        return T[b][:, o + r[1]:o + r[2]]
+        return T[b][:, o + r[1] + r[3]:o + r[2]:r[4]] if len(r) == 5 else T[b][:, o + r[1]:o + r[2]]
 
-    def back(b):
-        n, (b, o) = COLS[b], PLACE.get(b, (b, 0))
-        return T[b][:, o + n - 1:(o - 1 if o else None):-1]
+    def back(r):
+        r = reg(r)
+        b, o = PLACE.get(r[0], (r[0], 0))
+        return T[b][:, o + r[2] - 1:(o + r[1] - 1 if o + r[1] else None):-1]
 
     def src(x, rd):
         if isinstance(x, tuple) and len(x) == 2:
@@ -232,24 +311,24 @@ def rank_program(g, core, T, topo):
         rd = []
         x, y = src(a, rd), src(b, rd)
         op("V", lambda: V.tensor_tensor(out=v(o), in0=x, in1=y, op=f), rd, [reg(o)],
-           size(o) * (GATHER if inds(a, b) else 1 if any(psum(r[0]) for r in rd + [reg(o)]) else 2), 0.06 * inds(a, b))
+           size(o) * (GATHER if inds(a, b) else 1 if any(psum(r[0]) for r in rd) else 2), 0.05 * inds(a, b))
 
     def ts(o, a, s1, f0, s2=None, f1=None):
         rd = []
         x, y, z = src(a, rd), src(s1, rd), src(s2, rd)
         c = size(o) * (GATHER if inds(a) else 0.5 if small(o, a) else 1)
         if f1 is None:
-            op("V", lambda: V.tensor_scalar(out=v(o), in0=x, scalar1=y, scalar2=None, op0=f0), rd, [reg(o)], c)
+            op("V", lambda: V.tensor_scalar(out=v(o), in0=x, scalar1=y, scalar2=None, op0=f0), rd, [reg(o)], c, 0.05 * inds(a))
         else:
-            op("V", lambda: V.tensor_scalar(out=v(o), in0=x, scalar1=y, scalar2=z, op0=f0, op1=f1), rd, [reg(o)], c)
+            op("V", lambda: V.tensor_scalar(out=v(o), in0=x, scalar1=y, scalar2=z, op0=f0, op1=f1), rd, [reg(o)], c, 0.05 * inds(a))
 
     def cp(o, a):
         rd = []
         x = src(a, rd)
-        op("V", lambda: V.tensor_copy(out=v(o), in_=x), rd, [reg(o)], size(o) * (GATHER if inds(a) else 0.5 if small(o, a) else 1))
+        op("V", lambda: V.tensor_copy(out=v(o), in_=x), rd, [reg(o)], size(o) * (GATHER if inds(a) else 0.5 if small(o, a) else 1), 0.05 * inds(a))
 
     def scatter(win, lst, a):
-        op("V", lambda: V.tensor_copy(out=v(win).indirect(v(lst)), in_=v(a)), [reg(a), reg(lst)], [win], 3.8 * size(a))
+        op("V", lambda: V.tensor_copy(out=v(win).indirect(v(lst)), in_=v(a)), [reg(a), reg(lst)], [win], 3.8 * size(a), 0.05)
 
     def tr(o, a, f):
         op("V", lambda: V.tensor_reduce(out=v(o), in_=v(a), axis=AxisListType.X, op=f), [reg(a)], [reg(o)], size(a))
@@ -262,36 +341,35 @@ def rank_program(g, core, T, topo):
         rd, wr = [], [reg(o)]
         x, s, b = src(a, rd), src(scale, rd), src(bias, rd)
         if acc is None:
-            op("S", lambda: g.scalar.activation(out=v(o), in_=x, func=fn, bias=b, scale=s), rd, wr, size(o) * (GATHER if inds(a) else 1), 0.03)
+            op("S", lambda: g.scalar.activation(out=v(o), in_=x, func=fn, bias=b, scale=s), rd, wr, size(o) * (GATHER if inds(a) else 1), 0.065 * inds(a))
         else:
-            op("S", lambda: g.scalar.activation(out=v(o), in_=x, func=fn, bias=b, scale=s, accum_out=v(acc)), rd, wr + [reg(acc)], size(o), 0.05)
+            op("S", lambda: g.scalar.activation(out=v(o), in_=x, func=fn, bias=b, scale=s, accum_out=v(acc)), rd, wr + [reg(acc)], size(o), 0.02)
 
-    def mms(o, *pairs, start=True, stop=True, dep=()):
-        def one(j, l, r):
-            rap = T[r[0]][:, r[1] + r[3]:r[2]:r[4]] if len(r) == 5 else v(r)
-            return lambda: g.tensor.matmul(out=v(o), lhsT=v(l), rhs=rap, start=start and j == 0, stop=stop and j == len(pairs) - 1)
-        pairs = [(reg(l), reg(r)) for l, r in pairs]
-        four = 1 if pairs[0][1][0] in TWO else 4
-        return add("P", [one(j, l, r) for j, (l, r) in enumerate(pairs)], [p for l, r in pairs for p in (l, r[:3])], [reg(o)],
-                   max(64, size(o)) * four * len(pairs) * 0.5e-3, dep=dep)
+    def mms(o, *terms, start=True, stop=True, dep=()):
+        def one(j, l, r, w):
+            return lambda: g.tensor.matmul(out=v(w), lhsT=v(l), rhs=v(r), start=start and j == 0, stop=stop and j == len(terms) - 1)
+        terms = [(reg(x[0]), reg(x[1]), reg(x[2]) if len(x) > 2 else reg(o)) for x in terms]
+        cyc = sum(max(min(64, size(l)), size(r)) * (1 if r[0] in TWO else 4) for l, r, w in terms)
+        return add("P", [one(j, *x) for j, x in enumerate(terms)], [p[:3] for l, r, w in terms for p in (l, r)], [reg(o)], cyc * PE, dep=dep,
+                   grp=not (start and stop))
 
-    def iota(o, pattern, base, cm, small=False):
-        if small:
-            op("G", lambda: g.iota(v(o), pattern, base, cm, allow_small_or_imprecise_dtypes=True), [], [reg(o)], 2 * size(o), 0.13)
+    def iota(o, pattern, base, cm):
+        if PLACE.get(reg(o)[0], ("",))[0] == "all_int32":
+            op("G", lambda: g.iota(v(o), pattern, base, cm), [], [reg(o)], 0, 0.07 + 2 * size(o) * CYC)
         else:
-            op("G", lambda: g.iota(v(o), pattern, base, cm), [], [reg(o)], 2 * size(o), 0.13)
+            op("G", lambda: g.iota(v(o), pattern, base, cm, allow_small_or_imprecise_dtypes=True), [], [reg(o)], 0, 0.07 + 2 * size(o) * CYC)
 
-    def zero(o):
-        iota(o, [[0, size(o)]], 0, 0, reg(o)[0] not in ("UW", "FW", "KW"))
+    def fill(o, x=0):
+        iota(o, [[0, size(o)]], x, 0)
 
-    def rowsum(b, r, i, base=0):
-        return ((b, base + 15 - i, base + 143 - i), r + (i, 16))
+    def rowsum(b, r, base=0):
+        return [((b, base + 15 - i, base + 143 - i), reg(r) + (i, 16)) for i in range(16)]
 
-    def POOL(t, lo, hi):
-        return ("POOL", t * POOLW + lo, t * POOLW + hi)
+    def turned(w, r, o):
+        return [(reg(r) + (i, 16), w, reg(o) + (i, 16)) for i in range(16)]
 
     AND, SHR, ADD, SUB, MUL, MIN, MAX = Op.bitwise_and, Op.logical_shift_right, Op.add, Op.subtract, Op.mult, Op.min, Op.max
-    EQ, NE, GE, GT, LT, LE = Op.is_equal, Op.not_equal, Op.is_ge, Op.is_gt, Op.is_lt, Op.is_le
+    EQ, GE, GT, LT, LE = Op.is_equal, Op.is_ge, Op.is_gt, Op.is_lt, Op.is_le
 
     mate, far = T.cores[rank ^ 1], T.cores[rank ^ 4]
     fe = topo.engines(core, far)
@@ -305,30 +383,36 @@ def rank_program(g, core, T, topo):
 
     def send(sem, transfers, a, land):
         i = add("G", [lambda: g.remote_dma_fused(transfers, local_sem=T.sem.lsem)], [a], [], 1.0, sem="rem")
-        add("R", [], [], [land], 0.0, 2.2, sem, sent, (i,))
+        add("R", [], [], [land], 0.0, 2.0, sem, sent, (i,))
 
-    count(-1000)
-    for q, sem, b, x in (("Y", "dG", "GL", T.gd[:, :]), ("S", "dW", "wi", T.wt[:, :]), ("Y", "dX", "X:0:2048", T.xs[:, 0:2048]),
-                         ("S", "dX2", "X:2048:4096", T.xs[:, 2048:4096]), ("S", "dK", "ki", T.km[:, :]), ("S", "dT", "ti", T.th[:, :]),
-                         ("Y", "dR", "R0", T.xs[0:128:16, :])):
-        dma(q, sem, v(b), x, [], [reg(b)])
+    def OWN(t, lo=0, hi=S):
+        return ("OWN", t * OWNW + lo, t * OWNW + hi)
+
+    def ARP(t, lo, hi):
+        return ("ARP", t * ARPW + lo, t * ARPW + hi)
+
+    for q, sem, b, x, us in (("Y", "dG", "GL", T.gd[:, :], 3.0), ("S", "dW", "wi", T.wt[:, :], 2.0), ("Y", "dX", "X:0:2048", T.xs[:, 0:2048], 5.0),
+                             ("S", "dX2", "X:2048:4096", T.xs[:, 2048:4096], 5.0), ("S", "dK", "ki", T.km[:, :], 2.0),
+                             ("S", "dT", "ti", T.th[:, :], 2.0), ("Y", "dR", "R0", T.xs[0:128:16, :], 2.5)):
+        dma(q, sem, v(b), x, [], [reg(b)], us)
 
     iota("IP", [[0, 1]], 0, 1)
     iota("IZ", [[1, 144]], -15, 0)
     iota("IQ", [[1, 144]], 0, 0)
     iota("IJ", [[16, 80]], 0, 0)
-    iota("R48", [[1, 48]], 2049, 0, True)
-    iota("RI", [[1, 48]], 0, 0, True)
+    iota("R48", [[1, 48]], 2049, 0)
+    iota("RI", [[1, 48]], 0, 0)
+    iota("K2", [[1, 2]], 1, 0)
     iota("I256", [[1, 256]], 0, 0)
-    iota("IO", [[1, 256]], 0, 0, True)
-    iota("C2", [[2, 12], [0, 64]], 0, 0, True)
-    for b in ("UW:64:80", "FW:64:80", "KW:64:80", "Q:64:80", "ZER", "CB"):
-        zero(b)
-    for k in range(3):
-        iota(R("YB", k, k + 1), [[0, 1]], (-7000, -16000, -32000)[k], 0, True)
+    iota("IO", [[1, 256]], 0, 0)
+    iota("C2", [[2, 12], [0, 64]], 0, 0)
+    for b in ("UW:64:80", "FW:64:80", "KW:64:80", "MW:64:80", "Q:64:80", "KF:12:16", "UE:264:272", "ZER", "CB"):
+        fill(b)
+    fill("ONP", 4096)
+    fill("ONN", -4096)
     for t in range(RO):
-        zero(R("SND", 384 * t, 384 * t + 192))
-        zero(POOL(t, 192 + S, POOLW))
+        fill(R("SND", SNDW * t, SNDW * t + 144))
+        fill(OWN(t, S, S + CAP))
     IQ = "IQ:0:128"
     ts("IPa", "IP", 15, AND)
     ts("IPb", "IP", 4, SHR)
@@ -341,294 +425,283 @@ def rank_program(g, core, T, topo):
     ts("B", "IQa", "PG", EQ)
     cp("wf", "wi")
     cp("wb", "wi")
+    act("wn", "wf", Fn.Copy, scale=-1.0)
     mms("P3:0:3", ("B", "wb"))
-    for t in range(RO):
-        ts(R("ZW", 144 * t, 144 * t + 144), "Z1", R("wf", t, t + 1), MUL)
-    ts(POOL(0, 192, 192 + S), "GL", -255.0, ADD)
-    ts("SW", "P3:0:3", 255.0, MUL)
-    cp("KF", "ki")
+    ts("ZW:0:144", "Z1", "wf:0", MUL)
+    for t in range(1, RO):
+        act(R("ZW", 144 * t, 144 * t + 144), "Z1", Fn.Copy, scale=col("wn", t))
+    ts(OWN(0), "GL", -1.0, MUL, 255.0, ADD)
+    act("SW", "P3:0:3", Fn.Copy, scale=255.0)
+    cp("KF:0:12", "ki")
     ts("TH", "ti", 64.0, MUL)
+    ts("ID", IQ, "Pf", EQ)
+    ts("GI", "IQ:0:8", "PG", EQ, 64.0, MUL)
+    for o, a, s in (("Z64", "Z1", 64.0), ("ZN", "Z1", -64.0), ("ZP", "Z1", "PI"), ("GN8", "GI", -1.0), ("BF", "B", 1.0), ("NB", "B", -1.0),
+                    ("B2N", "B", -2.0), ("NI", "ID", -1.0), ("ID16", "ID", 16.0), ("ID8", "ID", 0.125), ("Y3", "ID", 1.5), ("Y1", "ID", -0.5),
+                    ("IDF", "ID", 1.0), ("IDB", "ID", 262144.0), ("tB", "ID", 1024.0), ("tD", "ID", 2048.0)):
+        act(o, a, Fn.Copy, scale=s)
+    ts("tA", IQ, "Pf", GT, -1.0, MUL)
+    ts("tC", IQ, "Pf", LT, -1.0, MUL)
+    ts("IQb", IQ, 15, AND)
+    ts("WI", "IQ:0:96", 15, AND)
+    tt("TN", "tA", "B", MUL)
+    tt("tC", "tC", "B", MUL)
+    tt("TS", "tB", "TN", ADD)
+    tt("TQ", "tD", "tC", ADD)
+    act("tB", "ID", Fn.Copy, scale=-4096.0)
+    tt("TS2", "tB", "TN", ADD)
+    ts("tA", "IQa", 16.0, MUL)
+    ts("B0", "tA", "Pf", EQ, 4.0, MUL)
+    ts("tA", IQ, 1.0, ADD, "Pf", EQ)
+    tt("SHF", "tA", "B", MUL)
+    ts("WM", "WI", "PI", EQ)
+    ts("SLW", "IJ", "PI", ADD)
+    ts("tA", "IQb", 1024.0, ADD)
+    tt("tC", "tA", "B", MUL)
+    ts("AG", "tC", -1024.0, ADD)
+    act("AG8", "AG", Fn.Copy, scale=256.0)
+    ts("tA", "IQb", -1024.0, ADD)
+    tt("tC", "tA", "B", MUL)
+    ts("AGp", "tC", 1024.0, ADD)
+    ts("P256", "PI", 256.0, MUL)
+    ts("H15", "PI", 15.0, EQ, 4095.0, MUL)
+    ts("IA", "IJ:0:64", 15.5, ADD)
+    act("IB", "IA", Fn.Copy, bias=-16.0)
+    act("SL24", "SLW:0:64", Fn.Copy, bias=24.0)
+    act("SLb", "SLW:0:16", Fn.Copy)
+    act("RBH", "SLW:0:3", Fn.Copy, bias=0.5)
+    act("RC", "SLW:0:3", Fn.Copy, scale=-1.0, bias=880.0)
+    act("SL6:0:3", "SLW:0:3", Fn.Copy)
+    act("SL6:3:6", "SLW:0:3", Fn.Copy)
+    ts("PL", "I256", "P256", ADD)
+    ts("BM", "I256:0:16", "PI", LE, 16384.0, MUL)
+    ts("LPI", "ZER:0:8", "PI", ADD)
+    tt("BK", ("KF", "LPI"), "BF", MUL)
 
     def prod(m):
-        b, o = ((6, 0), (7, 0), (1, 0), (1, 192))[m // 3]
-        return R("P%d" % b, o + 64 * (m % 3), o + 64 * (m % 3) + 64)
+        return R("P%d" % (6 + m % 2), 128 + 64 * (m // 2), 192 + 64 * (m // 2))
 
-    def ulist(t):
-        mms("P2:0:64", *[rowsum("ZW", POOL(t, 192, 192 + S), i, 144 * t) for i in range(16)])
-        ts("u0", "P2:0:64", R("SW", t, t + 1), ADD)
+    def lists(t):
+        mms("P2:0:64", *rowsum("ZW", OWN(t) if t else "GL", 144 * t))
+        if t:
+            ts("u0", "P2:0:64", col("SW", t), ADD)
+        else:
+            cp("u0", "P2:0:64")
         ts("UW:0:64", "u0", 4095, AND)
         cp("uf", "UW:0:64")
         tt("f0", "UW:0:64", "UW:0:64", MUL)
-        for m in range(M):
-            act(prod(m), "uf", Fn.Copy, scale=R("KF", m, m + 1))
         ts("FW:0:64", "f0", 5, SHR)
+        for m in range(M):
+            act(prod(m), "uf", Fn.Copy, scale=col("KF", m))
+        for a, b in CHUNKS:
+            for m in range(a, b):
+                tt(R("CI", 64 * m, 64 * m + 64), prod(m), "FW:0:64", ADD)
+            ts(R("CM", 64 * a, 64 * b), R("CI", 64 * a, 64 * b), 4095, AND)
+            cp(R("CL", 64 * a, 64 * b), R("CM", 64 * a, 64 * b))
+        for a in range(0, M, 4):
+            ts(R("BI", 64 * a, 64 * a + 256), R("CL", 64 * a, 64 * a + 256), 4000.0, GE)
 
-    def clist(j):
-        lo, hi = 192 * j, 192 * j + 192
-        for q in range(3):
-            tt(R("CI", lo + 64 * q, lo + 64 * q + 64), prod(3 * j + q), "FW:0:64", ADD)
-        ts(R("CM", lo, hi), R("CI", lo, hi), 4095, AND)
-        cp(R("CL", lo, hi), R("CM", lo, hi))
-        ts(R("BI", lo, hi), R("CL", lo, hi), 4000.0, GE)
+    def after(o, a, f, n, p):
+        act(f, "WM:0:16", Fn.Copy, scale=col(a, 0))
+        mms(p, ("IDF", "BM"), ("BF", f))
+        tr(n, p, MIN)
+        ts(o, a, n, MIN, 4095.0, MIN)
 
-    def consts1():
-        ts("ID", IQ, "Pf", EQ)
-        act("Z64", "Z1", Fn.Copy, scale=64.0)
-        act("Z128", "Z1", Fn.Copy, scale=128.0)
-        act("ZN", "Z1", Fn.Copy, scale=-64.0)
-
-    def consts2():
-        act("BF", "B", Fn.Copy)
-        act("NB", "B", Fn.Copy, scale=-1.0)
-        act("NI", "ID", Fn.Copy, scale=-1.0)
-        act("Y3", "ID", Fn.Copy, scale=1.5)
-        act("Y1", "ID", Fn.Copy, scale=-0.5)
-        ts("tA", IQ, "Pf", GT, -1.0, MUL)
-        ts("tC", IQ, "Pf", LT, -1.0, MUL)
-        ts("IQb", IQ, 15, AND)
-        ts("WI", "IQ:0:96", 15, AND)
-        act("tB", "ID", Fn.Copy, scale=1024.0)
-        tt("TN", "tA", "B", MUL)
-        tt("tC", "tC", "B", MUL)
-        ts("tA", "IQa", 16.0, MUL)
-        tt("TS", "tB", "TN", ADD)
-        act("tD", "ID", Fn.Copy, scale=2048.0)
-        ts("B0", "tA", "Pf", EQ, 4.0, MUL)
-        tt("TQ", "tD", "tC", ADD)
-        act("tE", "TN", Fn.Copy, scale=2.0)
-        ts("tA", "IQb", 1000.0, ADD)
-        tt("TG", "tE", "NI", ADD)
-        ts("WM", "WI", "PI", EQ)
-        tt("tC", "tA", "B", MUL)
-        ts("SLW", "IJ", "PI", ADD)
-        ts("AG", "tC", -1000.0, ADD)
-        ts("tA", "IQb", -1000.0, ADD)
-        act("IO16", "IO:0:64", Fn.Copy, scale=16.0)
-        tt("tA", "tA", "B", MUL)
-        ts("AGp", "tA", 1000.0, ADD)
-        ts("P256", "PI", 256.0, MUL)
-        ts("RBH", "SLW:0:3", 0.5, ADD)
-        ts("RC", "SLW:0:3", -1.0, MUL, 832.0, ADD)
-        ts("PL", "I256", "P256", ADD)
-        ts("BM", "I256:0:16", "PI", LE, 16384.0, MUL)
-        ts("EG:0", "PI", 3.0, GE, 5000.0, MUL)
-        ts("EG:1", "PI", 0.0, EQ, -1.0, MUL)
-        ts("EG:2", "PI", 1.0, GE, -1.0, MUL)
-        tt("junk:0:12", "WM:0:12", "KF", MUL)
-        tr("KD", "junk:0:12", ADD)
-
-    def utable():
-        ts("NK", "R0", 192.0, LT)
+    def tables():
+        act("NK", "R0", Fn.Sign, scale=-1.0, bias=191.5)
         scan("TU", "NK", "PL", 32768.0, MUL, MAX, True)
-        ts("fw", "WM:0:16", "TU:0", MUL)
-        mms("P7:0:16", ("BF", "fw"))
-        tt("junk:16:32", "P7:0:16", "BM", ADD)
-        tr("nf", "junk:16:32", MIN)
-        ts("UT", "TU", "nf", MIN, 4095.0, MIN)
+        after("UE:0:256", "TU", "fw", "nf", "P6:0:16")
+        mms("P6:16:24", ("SHF", "UE:0:8"))
+        act("UE:256:264", "P6:16:24", Fn.Identity, bias="H15")
+        scan("TE", "NK", "UE:8:264", 32768.0, MUL, MAX, True)
+        after(R("UE", E2, E2 + 256), "TE", "fw2", "nf2", "P6:32:48")
 
-    def three(f, o, w, a):
-        o, a = reg(o), reg(a)
-        for k in range(3):
-            f(sub(o, k, k + 1), sub(a, w * k, w * k + w))
-
-    def vsum(o, a):
-        tr(o, a, ADD)
-
-    def ssum(o, a):
-        act(R("junk", 64 * (o[1] % 3), 64 * (o[1] % 3) + 16), a, Fn.Copy, acc=o)
-
+    tables()
     for t in range(RO):
-        own = POOL(t, 192, 192 + S)
-        count(0)
-        ulist(t)
-        if t == 0:
-            k = count(-1000)
-            consts1()
-            count(k)
-        for j in range(4):
-            clist(j)
-        parts = {}
-        for b, m, n in ((0, 0, 6), (1, 6, 3), (6, 9, 3)):
-            parts[b] = [mms(R("P%d" % b, 0, 64 * n), *[("ID", R(x, 64 * m, 64 * (m + n))) for x in ("C2", "BI")], stop=False)]
+        own = OWN(t)
+        lists(t)
+        zs, last, keys = 0, {}, ["P0:448:512"]
         for m in range(M):
             Zm, Am, Cl = R("Z", S * m, S * m + S), R("A", S * m, S * m + S), R("CL", 64 * m, 64 * m + 64)
-            if m in SMS:
+            if KIND[m] == "S":
                 act(Zm, ("X", Cl), Fn.Copy)
                 for h in range(2):
-                    o, lo = "P%d" % (2 + h + 2 * (SMS.index(m) % 2)), 512 * h
-                    mms(o, ("ID", sub(own, lo, lo + 512)), ("ID", sub(Zm, lo, lo + 512)))
+                    o, lo = "P%d" % (2 + h + 2 * (zs % 2)), 512 * h
+                    mms(o, ("NI", sub(own, lo, lo + 512)), ("ID", sub(Zm, lo, lo + 512)))
                     act(sub(Am, lo, lo + 512), o, Fn.Abs)
+                zs += 1
             else:
-                tt(Zm, ("X", Cl), own, ADD)
-                if m in RMS:
-                    ts(Am, Zm, 0.0, MAX)
+                tt(Zm, ("X", Cl), own, SUB)
+                if KIND[m] == "V":
+                    ts(Am, Zm, 0.0, MAX, 2.0, MUL)
                 else:
                     act(Am, Zm, Fn.Abs)
-            b, n, last = (0, m, m == 5) if m < 6 else (1, m - 6, m == 8) if m < 9 else (6, m - 9, m == 11)
-            for z, x in (("ZN", Zm), ("Z128", Am)) if m in RMS else (("Z64", Am),):
-                stop = last and x is Am
-                parts[b].append(mms(R("P%d" % b, 64 * n, 64 * n + 64), *[rowsum(z, x, i) for i in range(16)],
-                                    start=False, stop=stop, dep=parts[b] if stop else ()))
-        if t == 0:
-            k = count(-1000)
-            consts2()
-            utable()
-            count(k)
-        cp("cur", "P0:0:192")
-        tt("cur", "cur", "P0:192:384", MIN)
-        tt("cur", "cur", "P1:0:192", MIN)
-        tt("cur", "cur", "P6:0:192", MIN)
-        tt("fa", "cur:0:64", "cur:64:128", MIN)
-        tt("KW:0:64", "fa", "cur:128:192", MIN)
+            if m < 2 * PAIRS:
+                if m % 2 == 0:
+                    continue
+                j = m // 2
+                o, n = R("P%d" % (j % 2), 128 * (j // 2), 128 * (j // 2) + 128), 128
+                sums = [turned(w, R(x, S * m - S, S * m + S), o) for w, x in (("GN8", "Z"), ("GI", "A"))]
+                head = [(R(x, 128 * j, 128 * j + 128), "ID") for x in ("C2", "BI")]
+            else:
+                j = m - 2 * PAIRS
+                o = R("P%d" % (6 + j % 2), 64 * (j // 2), 64 * (j // 2) + 64)
+                keys.append(o)
+                sums = [rowsum("ZN", Zm), rowsum("Z64", Am)]
+                head = [("ID", R(x, 64 * m, 64 * m + 64)) for x in ("C2", "BI")]
+            i = mms(o, *head, stop=False, dep=last.get(o[0], ()))
+            if KIND[m] == "V":
+                i = mms(o, *sums[0], start=False, stop=False, dep=(i,))
+            last[o[0]] = (mms(o, *sums[1], start=False, dep=(i,)),)
+        act("TM", "P0:0:128", Fn.Copy)
+        for j in range(1, PAIRS):
+            tt("TM", "TM", R("P%d" % (j % 2), 128 * (j // 2), 128 * (j // 2) + 128), MIN)
+        add("P", [lambda: g.tensor.transpose(v("P0:384:512"), v("TM"), v("IDF"))], [R("TM"), R("IDF")], [R("P0", 384, 512)], 512 * PE)
+        act("cur", "P0:384:448", Fn.Copy)
+        for x in keys[:-1]:
+            tt("cur", "cur", x, MIN)
+        tt("KW:0:64", "cur", keys[-1], MIN)
         ts("fb", "KW:0:64", 1, AND)
-        ts("fa", "KW:0:64", "TH", LT)
-        tt("FB", "fa", "fb", GT)
+        ts("P4:0:64", "KW:0:64", "TH", LT)
+        tt("FB", "P4:0:64", "fb", GT)
+        ts("MW:0:64", "KW:0:64", 1, SHR, 15, AND)
         mms("P2:0:64", ("B", "FB"))
         mms("P3:0:64", ("TQ", "FB"))
         scan("Cs", "P2:0:64", "ZER", 0.0, ADD, ADD)
         for k in range(3):
-            act(R("junk", 64 * k, 64 * k + 64), "Cs", Fn.Sign, scale=-1.0, bias=R("RBH", k, k + 1), acc=R("sA", k, k + 1))
+            act(R("junk", 64 * k, 64 * k + 64), "Cs", Fn.Sign, scale=-1.0, bias=col("RBH", k), acc=col("sA", k))
         tt("Q:0:64", "Cs", "P3:0:64", ADD)
-        ts("RV", "RI", "Cs:63", GE, 1048576.0, MUL)
-        ts("vl", "SLW:0:3", "Cs:63", LT)
-        tt("RV", "RV", "RI", ADD)
+        ts("RVi", "RI", "Cs:63", GE, 1048576.0, MUL)
+        ts("IV", "SL6", "Cs:63", GE, 8192.0, MUL)
         so = "sO:0:3"
         ts(so, "sA", 0.5, MUL, 32.0, ADD)
+        act("sob", "sA", Fn.Copy, scale=0.5, bias=32.0)
         tt("OH", ("Q", so), "R48", EQ)
-        tt("M1:0:48", ("KW", so), "OH", MUL)
-        mms("P4:0:48", ("BF", "M1:0:48"))
-        for j, b in enumerate(("UW", "FW", "SLW")):
-            tt(R("M1", 48 * j + 48, 48 * j + 96), (b, so), "OH", MUL)
-        mms("P5:0:144", ("BF", "M1:48:192"))
-        act("US", "P5:0:144", Fn.Copy)
-        cp("kI", "P4:0:48")
-        ts("mI", "kI", 1, SHR, 15, AND)
-        ts("dm", "kI", 0x7FFFC0, AND)
-        ts("xk", "mI", "PI", EQ, "KD", MUL)
-        mms("P6:0:48", ("BF", "xk"))
-        tt("CK:48:96", "dm", "RV", ADD)
-        tt("tk", "P6:0:48", "US:0:48", MUL)
-        tt("ts", "tk", "US:48:96", ADD)
-        ts("CK:0:48", "ts", 4095, AND)
-        tt("CKm", "CK", "WM", MUL)
-        three(ssum, "kw", 16, "CKm:48:96")
-        three(vsum, "cw", 16, "CKm:0:48")
-        ts("p1", "CK:0:48", 16.0, ADD)
-        ts("q1", "cw", 16.0, ADD)
-        ts("p1h", "p1", 8, SHR)
-        ts("q1l", "q1", 255, AND)
-        ts("sel", "p1h", "PI", EQ)
-        cp("qO:0:3", "q1l")
-        tt("T1", ("UT", "qO:0:3"), "sel", MUL)
-        mms("P7:0:48", ("BF", "T1"))
+        tt("M1:0:48", ("UW", so), "OH", MUL)
+        tt("M1:48:96", ("FW", so), "OH", MUL)
+        tt("Mm", ("MW", so), "OH", MUL)
+        tt("M1:96:144", ("KW", so), "OH", MUL)
+        mms("P4:0:48", ("BK", "M1:0:48"), ("BF", "M1:48:96"))
+        mms("P5:0:48", ("B", "Mm"))
+        ts("xi", "P4:0:48", 16.0, ADD)
+        ts("P5:0:48", "P5:0:48", "PI", EQ)
+        ts("xh", "xi", 0xF00, AND)
+        ts("xl", "xi", 255, AND)
+        tt("HL:0:48", "xh", "P5:0:48", MUL)
+        tt("HL:48:96", "xl", "P5:0:48", MUL)
+        mms("P7:0:96", ("B", "HL:0:48", "P7:0:48"), ("B", "HL:0:48", "P7:48:96"))
+        mms("P6:0:6", *rowsum("Z1", "HL"))
+        mms("P3:64:112", ("B", "HL:0:48"), ("B", "HL:48:96"))
+        mms("P2:64:112", ("ID", "RI"), ("ID", "RVi"), ("B2N", "Mm"), ("BF", "M1:96:144"))
+        act("CKk", "P2:64:112", Fn.Copy)
+        tt("KM", "P2:64:112", "WM:0:48", MUL)
         for k in range(3):
-            ts(R("tm", 48 * k, 48 * k + 48), "CK:0:48", R("cw", k, k + 1), NE, 2097152.0, MUL)
+            act(R("jk2", 16 * k, 16 * k + 16), R("KM", 16 * k, 16 * k + 16), Fn.Identity, bias=col("IV", k), acc=col("kw", k))
+        mms("P0:0:3", ("ID16", "sob"), *rowsum("ZP", "OH"))
+        act("swn", "P0:0:3", Fn.Copy, scale=-1.0, bias=-4096.0)
+        cp("sl16:0:3", "P0:0:3")
+        act("tg", (OWN(t, 0, S + 16), "sl16:0:3"), Fn.Copy)
+        cp("qO:0:3", "P6:3:6")
+        ts("qO:3:6", "P6:3:6", float(E2), ADD)
+        ts("sel", "P7:0:96", "P256", EQ)
+        act("WS", "P6:3:6", Fn.Copy, scale=-1.0)
+        tt("ncw", "WS", "P6:0:3", SUB)
+        tt("T2", ("UE", "qO:0:6"), "sel", MUL)
+        mms("P5:64:160", ("BF", "T2"))
+        tt("em", "P5:64:160", "WM", MUL)
         for k in range(3):
-            tt(R("tm", 48 * k, 48 * k + 48), R("tm", 48 * k, 48 * k + 48), "CK:48:96", ADD)
-        tt("em", "P7:0:48", "WM:0:48", MUL)
-        ts("p1", "P7:0:48", 8.0, ADD, 4095.0, MIN)
-        three(vsum, "ew:0:3", 16, "em")
-        ts("p1h", "p1", 8, SHR)
-        ts("q1", "ew:0:3", 8.0, ADD, 4095.0, MIN)
-        ts("sel", "p1h", "PI", EQ)
-        ts("q1l", "q1", 255, AND)
-        cp("qO:0:3", "q1l")
-        tt("T1", ("UT", "qO:0:3"), "sel", MUL)
-        mms("P7:0:48", ("BF", "T1"))
-        three(lambda o, a: tr(o, a, MIN), "mn", 48, "tm")
-        tt("eq", "mn", "kw", EQ)
-        tt("CB:2:5", "eq", "vl", MUL)
+            tr(col("ew", k), R("em", 16 * k, 16 * k + 16), ADD)
+            act(R("jk2", 64 + 16 * k, 80 + 16 * k), R("em", 48 + 16 * k, 64 + 16 * k), Fn.Copy, acc=col("ew", 3 + k))
+        ts("OFF:0:3", "ncw", -1.0, MUL, -6.0, ADD)
+        cp("OFF:3:9", "ew")
+        for k in range(3):
+            act(R("TK", 48 * k, 48 * k + 48), "P3:64:112", Fn.Abs, bias=col("ncw", k))
+        i = mms("P1:0:144", *[("IDF", "CKk", R("P1", 48 * k, 48 * k + 48)) for k in range(3)], stop=False)
+        mms("P1:0:144", ("IDB", "TK"), start=False, dep=(i,))
+        for k in range(3):
+            act(R("junk", 64 * k, 64 * k + 48), R("P1", 48 * k, 48 * k + 48), Fn.Relu, scale=-1.0, bias=col("kw", k), acc=col("lose", k))
+        act("CB:2:5", "lose", Fn.Relu, scale=-1.0, bias=1.0)
         mms("P3:0:1", ("B", "CB:2"), ("B", "CB:3"), ("B", "CB:4"))
         mms("P2:0:3", ("TS", "CB:2:5"), ("NB", "CB:1:4"), ("NB", "CB:0:3"))
-        ts("OFF:0:3", "cw", 10.0, ADD)
-        cp("OFF:3:6", "ew:0:3")
-        tt("em", "P7:0:48", "WM:0:48", MUL)
-        three(vsum, "ew:3:6", 16, "em")
-        cn = R("CN", t, t + 1)
-        cp(cn, "P3:0:1")
-        cp("OFF:6:9", "ew:3:6")
-        send("cn%d" % t, [transfer(far, fe, "cn%d" % t, cn, R("CNL", 2 * t + 1, 2 * t + 2)),
-                          transfer(mate, me, "cn%d" % t, cn, R("CNL", 2 * t, 2 * t + 1))], cn, R("CNL", 2 * t, 2 * t + 2))
-        cp("GX", ("X", "OFF:0:9"))
-        ts("GN", "GX", 0.0, MIN)
-        mms("P5:0:144", ("NI", "GX"), ("B0", "GN"))
+        mms("P0:8:11", ("TS2", "CB:2:5"), ("NB", "CB:1:4"), ("NB", "CB:0:3"))
+        cn = R("CN", 4 * t, 4 * t + 3)
+        ts(sub(cn, 0, 2), "K2", "P3:0:1", MUL)
+        ts(sub(cn, 2, 3), "P3:0:1", -1.0, MUL, 48.0, ADD)
+        n1, n2 = R("CNL", 8 * t, 8 * t + 3), R("CNL", 8 * t + 4, 8 * t + 7)
+        send("cn%d" % t, [transfer(far, fe, "cn%d" % t, cn, n2), transfer(mate, me, "cn%d" % t, cn, n1)], cn, R("CNL", 8 * t, 8 * t + 8))
+        act("GX", ("X", "OFF:0:9"), Fn.Copy)
+        act("GN", "GX", Fn.Relu, scale=-1.0)
+        mms("P4:64:208", ("ID", "GX"), ("B0", "GN"))
         tt("vv", "P2:0:3", "RC", MAX)
         for b in range(3):
-            ts(R("DL", 3 * b, 3 * b + 3), "vv", -1.0, MUL, 1024.0 + 64 * b, ADD)
-        tt("SLm", "US:96:144", "WM:0:48", MUL)
-        ts("GV", "P5:0:144", -255.0, MAX)
-        snd = R("SND", 384 * t, 384 * t + 384)
+            ts(R("DL", 3 * b, 3 * b + 3), "vv", -1.0, MUL, 1024.0 + CAP * b, ADD)
+        ts("GV", "P4:64:208", 255.0, MIN)
+        snd = R("SND", SNDW * t, SNDW * t + SNDW)
         scatter(snd, "DL:0:9", "GV")
-        send("ar%d" % t, [transfer(far, fe[:half], "ar%d" % t, sub(snd, 64, 128), POOL(t, 64, 128)),
-                          transfer(far, fe[half:], "ar%d" % t, sub(snd, 128, 192), POOL(t, 128, 192)),
-                          transfer(mate, me, "ar%d" % t, sub(snd, 0, 64), POOL(t, 0, 64))], snd, POOL(t, 0, 192))
-        three(ssum, "sw", 16, "SLm")
-        ts("nc", "CB:2:5", -100.0, MUL, 100.0, ADD)
-        cp("CE:0:3", "cw")
+        send("ar%d" % t, [transfer(far, fe[:half], "ar%d" % t, sub(snd, 48, 96), ARP(t, 48, 96)),
+                          transfer(far, fe[half:], "ar%d" % t, sub(snd, 96, 144), ARP(t, 96, 144)),
+                          transfer(mate, me, "ar%d" % t, sub(snd, 0, 48), ARP(t, 0, 48))], snd, ARP(t, 0, 144))
+        scatter(OWN(t, S, OWNW), "DL:0:3", "tg")
+        tt("pos", "P0:8:11", "swn", SUB)
+        tt("npos", "swn", "P0:8:11", SUB)
+        ts("posl", "pos", 15, AND)
+        cp("PF", "posl")
+        terms = []
+        for k in range(3):
+            for j, (tab, f, io) in enumerate((("AG", GE, "IA"), ("AGp", LT, "IB"))):
+                l, r = R("LL", 128 * (2 * k + j), 128 * (2 * k + j + 1)), R("SS", 64 * (2 * k + j), 64 * (2 * k + j + 1))
+                ts(l, tab, col("PF", k), f, 0.5, MUL)
+                act(r, io, Fn.Sign, bias=col("npos", k))
+                terms.append((l, r))
+        i = mms("P7:128:192", ("IDF", "SL24"), stop=False)
+        mms("P7:128:192", *terms, start=False, dep=(i,))
+        cp("LR", "P7:128:192")
+        cp(ARP(t, 144, 656), (OWN(t, 0, S + CAP), "LR:0:32"))
+        act(ARP(t, 656, ARPW), (OWN(t, 0, S + CAP), "LR:32:64"), Fn.Copy)
+        ts("CE:0:3", "ncw", -1.0, MUL, -16.0, ADD)
         ts("CE:3:6", "ew:3:6", 1.0, ADD)
-        ts("CE:12:18", "CE:0:6", 255, AND)
-        ts("CE:6:12", "CE:0:6", 8, SHR)
-        ts("CF:6:9", "CE:12:15", -1.0, MUL, 0.5, ADD)
-        ts("CF:9:12", "CE:15:18", 0.5, SUB)
-        tt("CF:0:3", "CE:6:9", "nc", ADD)
-        tt("CF:3:6", "CE:9:12", "nc", ADD)
-        LHk = [R("LH", 128 * k, 128 * k + 128) for k in range(8)]
-        RHk = [R("RH", 256 * k, 256 * k + 256) for k in range(6)]
+        ts("CE:6:12", "CE:0:6", 255, AND)
+        ts("CE:12:18", "CE:0:6", 0x1F00, AND)
+        ts("CFl", "CE:6:12", -1.0, MUL, 0.5, ADD)
+        tt("CFh", "CE:12:18", "IV", ADD)
+        terms = [("ID8", "ONP")]
         for k in range(6):
-            act(RHk[k], "IO", Fn.Sign, scale=1.0 if k < 3 else -1.0, bias=R("CF", 6 + k, 7 + k))
-            ts(LHk[k], "AG", R("CF", k, k + 1), EQ)
-        mms("P7:0:256", *zip(LHk, RHk))
-        cp("sl16:0:3", "sw")
-        cp("tg", (own, "sl16:0:3"))
-        scatter(POOL(t, 192 + S, POOLW), "DL:0:3", "tg")
-        ts("n5", "CB:2:5", -5000.0, MUL, 5000.0, ADD)
-        tt("pv", "sw", "vv", ADD)
-        tt("pv", "pv", "n5", ADD)
-        cp("lc", "P7:255")
-        mms("P3:0:1", ("TG", "lc"))
-        ts("P7:0:256", "P7:0:256", "P3:0:1", GT, -32768.0 / 2 ** t, MUL)
-        tt("R0", "R0", "P7:0:256", ADD)
+            l, lg, r = R("LH", 128 * k, 128 * k + 128), R("LG", 128 * k, 128 * k + 128), R("RH", 256 * k, 256 * k + 256)
+            act(r, "IO", Fn.Sign, bias=col("CFl", k))
+            act(lg, "AG8", Fn.Sign, scale=-1.0, bias=col("CFh", k))
+            ts(l, "AG8", col("CFh", k), EQ, -4096.0 if k < 3 else 4096.0, MUL)
+            terms += [(lg, "ONP" if k < 3 else "ONN"), (l, r)]
+        i = mms("P5:256:512", *terms[:7], stop=False)
+        mms("P5:256:512", *terms[7:], start=False, dep=(i,))
+        tt("R0", "R0", "P5:256:512", MIN)
         if t < RO - 1:
             dma("Y", "dM%d" % t, T.X[0:128:16, :], T.R0[:], [R("R0")], [R("X")])
-        n1, n2 = R("CNL", 2 * t, 2 * t + 1), R("CNL", 2 * t + 1, 2 * t + 2)
-        ts("ac:0", n2, 2.0, MUL, n1, ADD)
-        ts("ac:2", n2, "PI", MUL, "EG:0", ADD)
-        ts("ac:1", n1, "EG:1", MUL, 64.0, ADD)
-        ts("PO:0:3", "pv", "ac:0", ADD, -1024.0, ADD)
-        ts("PJ:0:3", "pv", "ac:0", ADD, -1024.0, ADD)
-        ts("PJ:3", "ac:2", n1, ADD)
-        ts("PO:3", "ac:2", n1, ADD)
-        ts("wt4", n2, "EG:2", MUL, "ac:1", ADD)
-        ts("PJ:4:8", "PJ:0:4", 15, AND)
-        cp("PF", "PJ:4:8")
-        pairs = []
-        for k in range(4):
-            a, b, pos, lo = sub(RHk[k], 0, 64), sub(RHk[k], 64, 128), R("PO", k, k + 1), R("PF", k, k + 1)
-            w = ("wt4", MUL) if k == 3 else ()
-            ts(a, "IO16", 15.0, ADD, pos, GE)
-            ts(b, "IO16", pos, GT)
-            ts(LHk[k], "AG", lo, GE, *w)
-            ts(LHk[4 + k], "AGp", lo, LT, *w)
-            pairs += [(LHk[k], a), (LHk[4 + k], b)]
-        mms("P6:0:64", *pairs)
-        tt("lf", "P6:0:64", "SLW:0:64", ADD)
-        cp("LST", "lf")
-        pool = POOL(t, 0, POOLW)
+        act(R("FY", 256 * t, 256 * t + 256), "R0", Fn.Sign, scale=-1.0, bias=-0.5)
+        ts("L2:10:65", "SLW:9:64", col(n1, 0), SUB, col(n2, 1), SUB)
+        ts("s1", "SLW:0:9", col(n1, 0), SUB)
+        ts("HT:0:9", "SLW:0:9", col(n1, 0), GE, col(n1, 2), MUL)
+        ts("HT:16:25", "s1", col(n2, 0), GE, col(n2, 2), MUL)
+        ts("HT:32:41", "s1", col(n2, 1), GE, col(n2, 2), MUL)
+        mms("P1:256:265", *[("ID", x) for x in ("SLb:0:9", "HT:0:9", "HT:16:25", "HT:32:41")])
+        cp("L2:0:9", "P1:256:265")
+        parts = ((144, 592, ARP(t, 144, ARPW), "L2:10:38"), (592, S, ARP(t, 144, ARPW), "L2:38:65"), (0, 144, ARP(t, 0, 288), "L2:0:9"))
         if t < RO - 1:
-            utable()
-            nxt = POOL(t + 1, 192, 192 + S)
-            cp(sub(nxt, 0, 512), (pool, "LST:0:32"))
-            act(sub(nxt, 512, 1024), (pool, "LST:32:64"), Fn.Copy)
+            tables()
+            for j, (lo, hi, win, l) in enumerate(parts):
+                if j == 1:
+                    act(OWN(t + 1, lo, hi), (win, l), Fn.Copy)
+                else:
+                    cp(OWN(t + 1, lo, hi), (win, l))
         else:
-            for k in range(3):
-                act(RHk[k], "R0", Fn.Sign, scale=-1.0, bias=R("YB", k, k + 1))
-            mms("P5:0:256", ("Y3", RHk[0]), ("Y1", RHk[1]), ("Y1", RHk[2]))
-            act("yct", "P5:0:256", Fn.Copy, bias=0.5)
+            mms("P6:0:256", ("Y1", "FY:0:256"), ("Y1", "FY:256:512"), ("Y3", "FY:512:768"))
+            act("yct", "P6:0:256", Fn.Copy, bias=0.5)
             dma("Y", "dC", T.yc[:, :], v("yct"), [R("yct")], [])
-            ts("YG:0:512", (pool, "LST:0:32"), 255.0, ADD)
-            act("YG:512:1024", (pool, "LST:32:64"), Fn.Copy, bias=255.0)
-            dma("Y", "dY0", T.yg[:, 0:512], T.YG[:, 0:512], [R("YG", 0, 512)], [])
-            dma("S", "dY1", T.yg[:, 512:1024], T.YG[:, 512:1024], [R("YG", 512, 1024)], [])
+            for j, (lo, hi, win, l) in enumerate(parts):
+                if j == 1:
+                    act(R("YG", lo, hi), (win, l), Fn.Copy, scale=-1.0, bias=255.0)
+                else:
+                    ts(R("YG", lo, hi), (win, l), -1.0, MUL, 255.0, ADD)
+                dma("S" if j == 1 else "Y", "dY%d" % j, T.yg[:, lo:hi], T.YG[:, lo:hi], [R("YG", lo, hi)], [])
     emit()
     g.wait_ge(T.sem.lsem, 2 * RO * sent)
     for e, n in list(cnt.items()) + [(d, 16) for d in LOADS]:

from concourse.bass import DstId, RemoteDMATransfer
from concourse.mybir import AluOpType as Op, AxisListType, ActivationFunctionType as Fn

RO, M, S, W, CAP = 3, 12, 1024, 4096, 48
OWNW, ARPW, SNDW = S + 192, 144 + S, 288
E2 = 272
_F32 = """wf 3 wn 3 KF 16 TH 1 SW 3 Pf 1 PI 1 PG 1 P16 1 P256 1 H15 1 K2 2 BF 128 BK 128 IDF 128 IDB 128 SHF 128 tA 128 tB 128 tC 128 tD 128
 WM 96 R48 48 SLW 80 SL6 6 SL24 64 IA 64 IB 64 RBH 3 RC 3 PL 256 BM 16 ZER 64 uf 64 Q 80 TM 128 cur 64 Cs 64 junk 192 jk2 192 sA 3 IV 6
 M1 144 CKk 48 KM 48 kw 3 WS 3 ncw 3 sel 96 T2 96 em 96 ew 6 TK 144 lose 3 vv 3 swn 3 npos 3 PF 3 s1 9 CFl 6 CFh 6
 UE 528 TU 256 TE 256 fw 16 fw2 16 nf 1 nf2 1 yct 256 CN 12 CNL 24"""
_BF = """X 4096 GL 1024 YG 1024 Z 12288 A 12288 wb 3 Z1 144 Z64 144 ZN 144 ZP 144 ZW 432 GI 8 GN8 8 B 128 NB 128 B2N 128 ID 128 NI 128 ID16 128
 ID8 128 TN 128 TS 128 TS2 128 TQ 128 B0 128 Y3 128 Y1 128 AG 128 AGp 128 AG8 128 IO 256 ONP 256 ONN 256 RI 48 SLb 16 BI 768 C2 768 FB 64
 OH 48 Mm 48 RVi 48 sob 3 HL 96 CB 8 GX 144 GN 144 GV 144 LH 768 LG 768 RH 1536 LL 768 SS 384 HT 48 R0 256 NK 256 FY 768 tg 48
 SND 864 OWN 3648 ARP 3504"""
_I32 = """wi 3 ki 12 ti 1 IP 1 IPa 1 IPb 1 IQ 144 IQa 128 IQb 128 IZ 144 IJ 80 I256 256 WI 96 UW 80 FW 80 KW 80 MW 80 u0 64 f0 64 CI 768 CM 768
 fb 64 xi 48 xh 48 xl 48 CE 18 pos 3 posl 3"""
_U16 = "CL 768 sO 4 DL 12 OFF 12 qO 8 LR 64 L2 66 sl16 4 LPI 8"
COLS, SCRATCH, PLACE = {}, {}, {}
for _txt, _dt in ((_F32, "float32"), (_BF, "bfloat16"), (_I32, "int32"), (_U16, "uint16")):
    _w, _at = _txt.split(), 16
    for _k in range(0, len(_w), 2):
        _n = int(_w[_k + 1])
        COLS[_w[_k]] = _n
        if _dt == "bfloat16" or _w[_k] in ("CN", "CNL"):
            SCRATCH[_w[_k]] = ("sbuf", [128, _n], _dt)
        else:
            PLACE[_w[_k]] = ("all_" + _dt, _at)
            _at += _n + (-_n) % 16
    if _dt != "bfloat16":
        SCRATCH["all_" + _dt] = ("sbuf", [128, _at], _dt)
for _b in range(8):
    SCRATCH["P%d" % _b] = ("psum", [128, 512], "float32")
    COLS["P%d" % _b] = 512
LOADS = ["dG", "dW", "dK", "dT", "dX", "dX2", "dR", "dM0", "dM1", "dY0", "dY1", "dY2", "dC"]
SEMAPHORES = ["sV", "sS", "sP", "sG", "lsem", "cn0", "cn1", "cn2", "ar0", "ar1", "ar2"] + LOADS

KIND = "SSVVSSVVVVSS"
PAIRS = 5
CHUNKS = ((0, 1), (1, 3), (3, 7), (7, 12))


def R(b, lo=0, hi=None):
    return (b, lo, COLS[b] if hi is None else hi)


def reg(x):
    if not isinstance(x, str):
        return x
    p = x.split(":")
    lo = int(p[1]) if len(p) > 1 else 0
    return (p[0], lo, int(p[2]) if len(p) > 2 else lo + 1 if len(p) > 1 else COLS[p[0]])


def sub(r, lo, hi):
    r = reg(r)
    return (r[0], r[1] + lo, r[1] + hi)


def col(r, k):
    return sub(r, k, k + 1)


WAKE, CYC, GATHER, PE, SLACK = 0.15, 1.04e-3, 1.56, 0.55e-3, 0.1
PASSES, STEPS, EASE = 4, 20000, 0.3
TWO = {_k for _t in (_BF, _U16) for _k in _t.split()}
ORDERS = {}


def psum(b):
    return b[0] == "P" and b[1:] in "01234567" and len(b) == 2


def links(nodes):
    hist, pre, bank = {}, [set() for _ in nodes], {}
    for i, x in enumerate(nodes):
        for regs, wr in ((x["rd"], False), (x["wr"], True)):
            for b, lo, hi in regs:
                for l, h, w, j in hist.get(b, ()):
                    if l < hi and lo < h and (w or wr):
                        pre[i].add(j)
        pre[i].update(x["dep"])
        if x["q"] == "P":
            group, since = bank.setdefault(x["wr"][0][0], ([], []))
            pre[i].update(group + since if x["grp"] else group)
            if x["grp"]:
                group[:], since[:] = [i], []
            else:
                since.append(i)
        pre[i].discard(i)
        for regs, wr in ((x["rd"], False), (x["wr"], True)):
            for b, lo, hi in regs:
                h = hist.setdefault(b, [])
                if wr:
                    h[:] = [e for e in h if not (lo <= e[0] and e[1] <= hi)]
                h.append((lo, hi, wr, i))
    return pre


def lay(nodes, pre, suc, prio):
    n = len(nodes)
    left, rdy, end, ready, free, order = [len(p) for p in pre], [0.0] * n, [0.0] * n, {}, {}, []
    for i in range(n):
        if not left[i]:
            ready.setdefault(nodes[i]["q"], []).append(i)
    while len(order) < n:
        best = None
        for q, l in ready.items():
            if l:
                f = free.get(q, 0.0)
                t = max(f, min(rdy[i] for i in l)) + SLACK
                i = max((i for i in l if rdy[i] <= t), key=lambda i: (prio[i], -i))
                if best is None or max(f, rdy[i]) < best[0]:
                    best = (max(f, rdy[i]), q, i)
        s, q, i = best
        ready[q].remove(i)
        order.append(i)
        if q != "R":
            free[q] = s + nodes[i]["dur"]
        end[i] = s + nodes[i]["dur"] + nodes[i]["lat"]
        for j in suc[i]:
            rdy[j] = max(rdy[j], end[i] + WAKE)
            left[j] -= 1
            if not left[j]:
                ready.setdefault(nodes[j]["q"], []).append(j)
    return order, end


def plan(nodes):
    n, pre = len(nodes), links(nodes)
    suc = [[] for _ in nodes]
    for i in range(n):
        for j in pre[i]:
            suc[j].append(i)
    qs, dur, lat = [x["q"] for x in nodes], [x["dur"] for x in nodes], [x["lat"] for x in nodes]
    need = [[(j, 0.0 if qs[i] == qs[j] == "P" else WAKE) for j in pre[i]] for i in range(n)]
    banks = [sorted({r[0] for r in x["rd"] + x["wr"] if psum(r[0])}) for x in nodes]

    def run(order):
        end, why, free, held = [0.0] * n, [None] * n, {}, {"P%d" % b: {} for b in range(8)}
        for i in order:
            s, w, q = 0.0, None, qs[i]
            for j, d in need[i]:
                if end[j] + d > s:
                    s, w = end[j] + d, (j, True)
            f = free.get(q)
            if f is not None and end[f] - lat[f] > s:
                s, w = end[f] - lat[f], (f, False)
            for b in banks[i]:
                for p, j in held[b].items():
                    if p != q and end[j] + WAKE > s:
                        s, w = end[j] + WAKE, (j, False)
                held[b][q] = i
            end[i], why[i] = s + dur[i] + lat[i], w
            if q != "R":
                free[q] = i
        e = max(end)
        return e, why, end.index(e), order

    def swap(order, j, i, early):
        a, b = order.index(j), order.index(i)
        part, move = order[a:b + 1], {i if early else j}
        for k in (reversed(part) if early else part):
            if k in move:
                move.update(pre[k] if early else suc[k])
        if (j if early else i) in move:
            return None
        go, stay = [k for k in part if k in move], [k for k in part if k not in move]
        return order[:a] + (go + stay if early else stay + go) + order[b + 1:]

    prio = [0.0] * n
    for i in range(n - 1, -1, -1):
        prio[i] = dur[i] + lat[i] + max([prio[j] + WAKE for j in suc[i]], default=0.0)
    tries = []
    for _ in range(PASSES):
        order, end = lay(nodes, pre, suc, prio)
        tries.append(run(order))
        prio = lay(nodes, suc, pre, end)[1]
    cur = best = min(tries, key=lambda x: x[0])
    seed = 1
    for step in range(STEPS):
        chain, i = [], cur[2]
        while cur[1][i]:
            chain.append((i, cur[1][i][1]))
            i = cur[1][i][0]
        chain.append((i, True))
        spots = [k for k, x in enumerate(chain) if not x[1]]
        seed = (seed * 1103515245 + 12345) % 2147483648
        a = b = spots[(seed >> 8) % len(spots)]
        for _ in range((seed >> 24) % 4):
            b += not chain[b + 1][1]
        new = swap(cur[3], chain[b + 1][0], chain[a][0], seed >> 29 & 1)
        if new:
            new = run(new)
            if new[0] < cur[0] + EASE * (1 - step / STEPS) * ((seed >> 4) % 16) / 16:
                cur = new
                if cur[0] < best[0]:
                    best = cur
    ORDERS["end"] = best[:3] + (nodes,)
    return best[3]


def builder(g, T):
    eng = {"V": g.vector, "S": g.scalar, "P": g.tensor, "G": g, "Y": g.sync}
    cnt = {"V": 0, "S": 0, "P": 0, "G": 0}
    know = {q: {} for q in eng}
    snap = {}
    hist = {}
    nodes = []

    def wait(q, reads, writes):
        want = {}
        for regs, wr in ((reads, False), (writes, True)):
            for b, lo, hi in regs:
                ps = psum(b)
                for h in hist.get(b, ()):
                    same = h[3] == q
                    if same and q == "P":
                        continue
                    over = h[0] < hi and lo < h[1]
                    if ((ps and not same) or (over and (h[2] or wr))) and want.get(h[3], 0) < h[4]:
                        want[h[3]] = h[4]
        for e, c in sorted(want.items(), key=lambda x: (x[0] == q, x[0])):
            k = know[q]
            if k.get(e, 0) < c:
                eng[q].wait_ge(T.sem["s" + e if e in cnt else e], c)
                for e2, c2 in list(snap.get((e, c), {}).items()) + [(e, c)]:
                    if k.get(e2, 0) < c2:
                        k[e2] = c2

    def log(reads, writes, e, c):
        for regs, wr in ((reads, False), (writes, True)):
            for b, lo, hi in regs:
                h = hist.setdefault(b, [])
                h[:] = [x for x in h if not (lo <= x[0] and x[1] <= hi and
                                             ((x[3] == e and x[2] == wr) or (wr and not psum(b))))]
                h.append([lo, hi, wr, e, c])

    def add(q, calls, rd, wr, dur, lat=0.0, sem=None, val=16, dep=(), grp=False):
        nodes.append({"q": q, "calls": calls, "rd": rd, "wr": wr, "dur": dur, "lat": lat, "sem": sem, "val": val, "dep": tuple(dep), "grp": grp})
        return len(nodes) - 1

    def emit():
        if "order" not in ORDERS:
            ORDERS["order"] = plan(nodes)
        for i in ORDERS["order"]:
            x = nodes[i]
            q, sem = x["q"], x["sem"]
            if q == "R":
                log([], x["wr"], sem, x["val"])
                continue
            wait(q, x["rd"], x["wr"])
            for j, call in enumerate(x["calls"]):
                ins = call()
                if sem is None and j == len(x["calls"]) - 1:
                    ins.then_inc(T.sem["s" + q], 1)
                    cnt[q] += 1
                    snap[(q, cnt[q])] = dict(know[q])
                    log(x["rd"], x["wr"], q, cnt[q])
                elif sem is not None and sem[0] == "d":
                    ins.then_inc(T.sem[sem], 16)
                    snap[(sem, 16)] = dict(know[q])
                    log(x["rd"], x["wr"], sem, 16)

    return add, emit, cnt


def rank_program(g, core, T, topo):
    rank = T.rank_of(core)
    if rank is None:
        return
    add, emit, cnt = builder(g, T)
    V = g.vector

    def op(q, call, rd, wr, cycles, plus=0.0):
        add(q, [call], rd, wr, plus + max(64, cycles) * CYC)

    def dma(q, sem, out, in_, rd, wr, us=2.5):
        add(q, [lambda: (g.sync if q == "Y" else g.scalar).dma_start(out=out, in_=in_)], rd, wr, 0.1, us, sem)

    def size(r):
        r = reg(r)
        return r[2] - r[1] if len(r) == 3 else (r[2] - r[1]) // r[4]

    def inds(*xs):
        return any(isinstance(x, tuple) and len(x) == 2 for x in xs)

    def small(*xs):
        return all(reg(x)[0] in TWO for x in xs)

    def v(r):
        r = reg(r)
        b, o = PLACE.get(r[0], (r[0], 0))
        return T[b][:, o + r[1] + r[3]:o + r[2]:r[4]] if len(r) == 5 else T[b][:, o + r[1]:o + r[2]]

    def back(r):
        r = reg(r)
        b, o = PLACE.get(r[0], (r[0], 0))
        return T[b][:, o + r[2] - 1:(o + r[1] - 1 if o + r[1] else None):-1]

    def src(x, rd):
        if isinstance(x, tuple) and len(x) == 2:
            a, b = reg(x[0]), reg(x[1])
            rd += [a, b]
            return v(a).indirect(v(b))
        if isinstance(x, (tuple, str)):
            rd.append(reg(x))
            return v(x)
        return x

    def tt(o, a, b, f):
        rd = []
        x, y = src(a, rd), src(b, rd)
        op("V", lambda: V.tensor_tensor(out=v(o), in0=x, in1=y, op=f), rd, [reg(o)],
           size(o) * (GATHER if inds(a, b) else 1 if any(psum(r[0]) for r in rd) else 2), 0.05 * inds(a, b))

    def ts(o, a, s1, f0, s2=None, f1=None):
        rd = []
        x, y, z = src(a, rd), src(s1, rd), src(s2, rd)
        c = size(o) * (GATHER if inds(a) else 0.5 if small(o, a) else 1)
        if f1 is None:
            op("V", lambda: V.tensor_scalar(out=v(o), in0=x, scalar1=y, scalar2=None, op0=f0), rd, [reg(o)], c, 0.05 * inds(a))
        else:
            op("V", lambda: V.tensor_scalar(out=v(o), in0=x, scalar1=y, scalar2=z, op0=f0, op1=f1), rd, [reg(o)], c, 0.05 * inds(a))

    def cp(o, a):
        rd = []
        x = src(a, rd)
        op("V", lambda: V.tensor_copy(out=v(o), in_=x), rd, [reg(o)], size(o) * (GATHER if inds(a) else 0.5 if small(o, a) else 1), 0.05 * inds(a))

    def scatter(win, lst, a):
        op("V", lambda: V.tensor_copy(out=v(win).indirect(v(lst)), in_=v(a)), [reg(a), reg(lst)], [win], 3.8 * size(a), 0.05)

    def tr(o, a, f):
        op("V", lambda: V.tensor_reduce(out=v(o), in_=v(a), axis=AxisListType.X, op=f), [reg(a)], [reg(o)], size(a))

    def scan(o, a, b, ini, f0, f1, turn=False):
        w = back if turn else v
        op("V", lambda: V.tensor_tensor_scan(out=w(o), data0=w(a), data1=w(b), initial=ini, op0=f0, op1=f1), [reg(a), reg(b)], [reg(o)], size(o))

    def act(o, a, fn, scale=1.0, bias=0.0, acc=None):
        rd, wr = [], [reg(o)]
        x, s, b = src(a, rd), src(scale, rd), src(bias, rd)
        if acc is None:
            op("S", lambda: g.scalar.activation(out=v(o), in_=x, func=fn, bias=b, scale=s), rd, wr, size(o) * (GATHER if inds(a) else 1), 0.065 * inds(a))
        else:
            op("S", lambda: g.scalar.activation(out=v(o), in_=x, func=fn, bias=b, scale=s, accum_out=v(acc)), rd, wr + [reg(acc)], size(o), 0.02)

    def mms(o, *terms, start=True, stop=True, dep=()):
        def one(j, l, r, w):
            return lambda: g.tensor.matmul(out=v(w), lhsT=v(l), rhs=v(r), start=start and j == 0, stop=stop and j == len(terms) - 1)
        terms = [(reg(x[0]), reg(x[1]), reg(x[2]) if len(x) > 2 else reg(o)) for x in terms]
        cyc = sum(max(min(64, size(l)), size(r)) * (1 if r[0] in TWO else 4) for l, r, w in terms)
        return add("P", [one(j, *x) for j, x in enumerate(terms)], [p[:3] for l, r, w in terms for p in (l, r)], [reg(o)], cyc * PE, dep=dep,
                   grp=not (start and stop))

    def iota(o, pattern, base, cm):
        if PLACE.get(reg(o)[0], ("",))[0] == "all_int32":
            op("G", lambda: g.iota(v(o), pattern, base, cm), [], [reg(o)], 0, 0.07 + 2 * size(o) * CYC)
        else:
            op("G", lambda: g.iota(v(o), pattern, base, cm, allow_small_or_imprecise_dtypes=True), [], [reg(o)], 0, 0.07 + 2 * size(o) * CYC)

    def fill(o, x=0):
        iota(o, [[0, size(o)]], x, 0)

    def rowsum(b, r, base=0):
        return [((b, base + 15 - i, base + 143 - i), reg(r) + (i, 16)) for i in range(16)]

    def turned(w, r, o):
        return [(reg(r) + (i, 16), w, reg(o) + (i, 16)) for i in range(16)]

    AND, SHR, ADD, SUB, MUL, MIN, MAX = Op.bitwise_and, Op.logical_shift_right, Op.add, Op.subtract, Op.mult, Op.min, Op.max
    EQ, GE, GT, LT, LE = Op.is_equal, Op.is_ge, Op.is_gt, Op.is_lt, Op.is_le

    mate, far = T.cores[rank ^ 1], T.cores[rank ^ 4]
    fe = topo.engines(core, far)
    me = [e for e in topo.engines(core, mate) if e not in fe][:len(fe)]
    half = len(fe) // 2

    def transfer(dst, es, sem, a, b):
        rid, pid = topo.addr(dst, core)
        return RemoteDMATransfer(dst_ids=[DstId(rid=rid, pnc=pid)], dma_engine_mask=sum(1 << e for e in es), remote_sem=T.sem[sem], src=v(a), dst=v(b))
    sent = len(fe) + len(me)

    def send(sem, transfers, a, land):
        i = add("G", [lambda: g.remote_dma_fused(transfers, local_sem=T.sem.lsem)], [a], [], 1.0, sem="rem")
        add("R", [], [], [land], 0.0, 2.0, sem, sent, (i,))

    def OWN(t, lo=0, hi=S):
        return ("OWN", t * OWNW + lo, t * OWNW + hi)

    def ARP(t, lo, hi):
        return ("ARP", t * ARPW + lo, t * ARPW + hi)

    for q, sem, b, x, us in (("Y", "dG", "GL", T.gd[:, :], 3.0), ("S", "dW", "wi", T.wt[:, :], 2.0), ("Y", "dX", "X:0:2048", T.xs[:, 0:2048], 5.0),
                             ("S", "dX2", "X:2048:4096", T.xs[:, 2048:4096], 5.0), ("S", "dK", "ki", T.km[:, :], 2.0),
                             ("S", "dT", "ti", T.th[:, :], 2.0), ("Y", "dR", "R0", T.xs[0:128:16, :], 2.5)):
        dma(q, sem, v(b), x, [], [reg(b)], us)

    iota("IP", [[0, 1]], 0, 1)
    iota("IZ", [[1, 144]], -15, 0)
    iota("IQ", [[1, 144]], 0, 0)
    iota("IJ", [[16, 80]], 0, 0)
    iota("R48", [[1, 48]], 2049, 0)
    iota("RI", [[1, 48]], 0, 0)
    iota("K2", [[1, 2]], 1, 0)
    iota("I256", [[1, 256]], 0, 0)
    iota("IO", [[1, 256]], 0, 0)
    iota("C2", [[2, 12], [0, 64]], 0, 0)
    for b in ("UW:64:80", "FW:64:80", "KW:64:80", "MW:64:80", "Q:64:80", "KF:12:16", "UE:264:272", "ZER", "CB"):
        fill(b)
    fill("ONP", 4096)
    fill("ONN", -4096)
    for t in range(RO):
        fill(R("SND", SNDW * t, SNDW * t + 144))
        fill(OWN(t, S, S + CAP))
    IQ = "IQ:0:128"
    ts("IPa", "IP", 15, AND)
    ts("IPb", "IP", 4, SHR)
    cp("Pf", "IP")
    cp("PG", "IPb")
    cp("PI", "IPa")
    ts("P16", "PG", 16.0, MUL)
    ts("IQa", IQ, 4, SHR)
    ts("Z1", "IZ", "P16", EQ)
    ts("B", "IQa", "PG", EQ)
    cp("wf", "wi")
    cp("wb", "wi")
    act("wn", "wf", Fn.Copy, scale=-1.0)
    mms("P3:0:3", ("B", "wb"))
    ts("ZW:0:144", "Z1", "wf:0", MUL)
    for t in range(1, RO):
        act(R("ZW", 144 * t, 144 * t + 144), "Z1", Fn.Copy, scale=col("wn", t))
    ts(OWN(0), "GL", -1.0, MUL, 255.0, ADD)
    act("SW", "P3:0:3", Fn.Copy, scale=255.0)
    cp("KF:0:12", "ki")
    ts("TH", "ti", 64.0, MUL)
    ts("ID", IQ, "Pf", EQ)
    ts("GI", "IQ:0:8", "PG", EQ, 64.0, MUL)
    for o, a, s in (("Z64", "Z1", 64.0), ("ZN", "Z1", -64.0), ("ZP", "Z1", "PI"), ("GN8", "GI", -1.0), ("BF", "B", 1.0), ("NB", "B", -1.0),
                    ("B2N", "B", -2.0), ("NI", "ID", -1.0), ("ID16", "ID", 16.0), ("ID8", "ID", 0.125), ("Y3", "ID", 1.5), ("Y1", "ID", -0.5),
                    ("IDF", "ID", 1.0), ("IDB", "ID", 262144.0), ("tB", "ID", 1024.0), ("tD", "ID", 2048.0)):
        act(o, a, Fn.Copy, scale=s)
    ts("tA", IQ, "Pf", GT, -1.0, MUL)
    ts("tC", IQ, "Pf", LT, -1.0, MUL)
    ts("IQb", IQ, 15, AND)
    ts("WI", "IQ:0:96", 15, AND)
    tt("TN", "tA", "B", MUL)
    tt("tC", "tC", "B", MUL)
    tt("TS", "tB", "TN", ADD)
    tt("TQ", "tD", "tC", ADD)
    act("tB", "ID", Fn.Copy, scale=-4096.0)
    tt("TS2", "tB", "TN", ADD)
    ts("tA", "IQa", 16.0, MUL)
    ts("B0", "tA", "Pf", EQ, 4.0, MUL)
    ts("tA", IQ, 1.0, ADD, "Pf", EQ)
    tt("SHF", "tA", "B", MUL)
    ts("WM", "WI", "PI", EQ)
    ts("SLW", "IJ", "PI", ADD)
    ts("tA", "IQb", 1024.0, ADD)
    tt("tC", "tA", "B", MUL)
    ts("AG", "tC", -1024.0, ADD)
    act("AG8", "AG", Fn.Copy, scale=256.0)
    ts("tA", "IQb", -1024.0, ADD)
    tt("tC", "tA", "B", MUL)
    ts("AGp", "tC", 1024.0, ADD)
    ts("P256", "PI", 256.0, MUL)
    ts("H15", "PI", 15.0, EQ, 4095.0, MUL)
    ts("IA", "IJ:0:64", 15.5, ADD)
    act("IB", "IA", Fn.Copy, bias=-16.0)
    act("SL24", "SLW:0:64", Fn.Copy, bias=24.0)
    act("SLb", "SLW:0:16", Fn.Copy)
    act("RBH", "SLW:0:3", Fn.Copy, bias=0.5)
    act("RC", "SLW:0:3", Fn.Copy, scale=-1.0, bias=880.0)
    act("SL6:0:3", "SLW:0:3", Fn.Copy)
    act("SL6:3:6", "SLW:0:3", Fn.Copy)
    ts("PL", "I256", "P256", ADD)
    ts("BM", "I256:0:16", "PI", LE, 16384.0, MUL)
    ts("LPI", "ZER:0:8", "PI", ADD)
    tt("BK", ("KF", "LPI"), "BF", MUL)

    def prod(m):
        return R("P%d" % (6 + m % 2), 128 + 64 * (m // 2), 192 + 64 * (m // 2))

    def lists(t):
        mms("P2:0:64", *rowsum("ZW", OWN(t) if t else "GL", 144 * t))
        if t:
            ts("u0", "P2:0:64", col("SW", t), ADD)
        else:
            cp("u0", "P2:0:64")
        ts("UW:0:64", "u0", 4095, AND)
        cp("uf", "UW:0:64")
        tt("f0", "UW:0:64", "UW:0:64", MUL)
        ts("FW:0:64", "f0", 5, SHR)
        for m in range(M):
            act(prod(m), "uf", Fn.Copy, scale=col("KF", m))
        for a, b in CHUNKS:
            for m in range(a, b):
                tt(R("CI", 64 * m, 64 * m + 64), prod(m), "FW:0:64", ADD)
            ts(R("CM", 64 * a, 64 * b), R("CI", 64 * a, 64 * b), 4095, AND)
            cp(R("CL", 64 * a, 64 * b), R("CM", 64 * a, 64 * b))
        for a in range(0, M, 4):
            ts(R("BI", 64 * a, 64 * a + 256), R("CL", 64 * a, 64 * a + 256), 4000.0, GE)

    def after(o, a, f, n, p):
        act(f, "WM:0:16", Fn.Copy, scale=col(a, 0))
        mms(p, ("IDF", "BM"), ("BF", f))
        tr(n, p, MIN)
        ts(o, a, n, MIN, 4095.0, MIN)

    def tables():
        act("NK", "R0", Fn.Sign, scale=-1.0, bias=191.5)
        scan("TU", "NK", "PL", 32768.0, MUL, MAX, True)
        after("UE:0:256", "TU", "fw", "nf", "P6:0:16")
        mms("P6:16:24", ("SHF", "UE:0:8"))
        act("UE:256:264", "P6:16:24", Fn.Identity, bias="H15")
        scan("TE", "NK", "UE:8:264", 32768.0, MUL, MAX, True)
        after(R("UE", E2, E2 + 256), "TE", "fw2", "nf2", "P6:32:48")

    tables()
    for t in range(RO):
        own = OWN(t)
        lists(t)
        zs, last, keys = 0, {}, ["P0:448:512"]
        for m in range(M):
            Zm, Am, Cl = R("Z", S * m, S * m + S), R("A", S * m, S * m + S), R("CL", 64 * m, 64 * m + 64)
            if KIND[m] == "S":
                act(Zm, ("X", Cl), Fn.Copy)
                for h in range(2):
                    o, lo = "P%d" % (2 + h + 2 * (zs % 2)), 512 * h
                    mms(o, ("NI", sub(own, lo, lo + 512)), ("ID", sub(Zm, lo, lo + 512)))
                    act(sub(Am, lo, lo + 512), o, Fn.Abs)
                zs += 1
            else:
                tt(Zm, ("X", Cl), own, SUB)
                if KIND[m] == "V":
                    ts(Am, Zm, 0.0, MAX, 2.0, MUL)
                else:
                    act(Am, Zm, Fn.Abs)
            if m < 2 * PAIRS:
                if m % 2 == 0:
                    continue
                j = m // 2
                o, n = R("P%d" % (j % 2), 128 * (j // 2), 128 * (j // 2) + 128), 128
                sums = [turned(w, R(x, S * m - S, S * m + S), o) for w, x in (("GN8", "Z"), ("GI", "A"))]
                head = [(R(x, 128 * j, 128 * j + 128), "ID") for x in ("C2", "BI")]
            else:
                j = m - 2 * PAIRS
                o = R("P%d" % (6 + j % 2), 64 * (j // 2), 64 * (j // 2) + 64)
                keys.append(o)
                sums = [rowsum("ZN", Zm), rowsum("Z64", Am)]
                head = [("ID", R(x, 64 * m, 64 * m + 64)) for x in ("C2", "BI")]
            i = mms(o, *head, stop=False, dep=last.get(o[0], ()))
            if KIND[m] == "V":
                i = mms(o, *sums[0], start=False, stop=False, dep=(i,))
            last[o[0]] = (mms(o, *sums[1], start=False, dep=(i,)),)
        act("TM", "P0:0:128", Fn.Copy)
        for j in range(1, PAIRS):
            tt("TM", "TM", R("P%d" % (j % 2), 128 * (j // 2), 128 * (j // 2) + 128), MIN)
        add("P", [lambda: g.tensor.transpose(v("P0:384:512"), v("TM"), v("IDF"))], [R("TM"), R("IDF")], [R("P0", 384, 512)], 512 * PE)
        act("cur", "P0:384:448", Fn.Copy)
        for x in keys[:-1]:
            tt("cur", "cur", x, MIN)
        tt("KW:0:64", "cur", keys[-1], MIN)
        ts("fb", "KW:0:64", 1, AND)
        ts("P4:0:64", "KW:0:64", "TH", LT)
        tt("FB", "P4:0:64", "fb", GT)
        ts("MW:0:64", "KW:0:64", 1, SHR, 15, AND)
        mms("P2:0:64", ("B", "FB"))
        mms("P3:0:64", ("TQ", "FB"))
        scan("Cs", "P2:0:64", "ZER", 0.0, ADD, ADD)
        for k in range(3):
            act(R("junk", 64 * k, 64 * k + 64), "Cs", Fn.Sign, scale=-1.0, bias=col("RBH", k), acc=col("sA", k))
        tt("Q:0:64", "Cs", "P3:0:64", ADD)
        ts("RVi", "RI", "Cs:63", GE, 1048576.0, MUL)
        ts("IV", "SL6", "Cs:63", GE, 8192.0, MUL)
        so = "sO:0:3"
        ts(so, "sA", 0.5, MUL, 32.0, ADD)
        act("sob", "sA", Fn.Copy, scale=0.5, bias=32.0)
        tt("OH", ("Q", so), "R48", EQ)
        tt("M1:0:48", ("UW", so), "OH", MUL)
        tt("M1:48:96", ("FW", so), "OH", MUL)
        tt("Mm", ("MW", so), "OH", MUL)
        tt("M1:96:144", ("KW", so), "OH", MUL)
        mms("P4:0:48", ("BK", "M1:0:48"), ("BF", "M1:48:96"))
        mms("P5:0:48", ("B", "Mm"))
        ts("xi", "P4:0:48", 16.0, ADD)
        ts("P5:0:48", "P5:0:48", "PI", EQ)
        ts("xh", "xi", 0xF00, AND)
        ts("xl", "xi", 255, AND)
        tt("HL:0:48", "xh", "P5:0:48", MUL)
        tt("HL:48:96", "xl", "P5:0:48", MUL)
        mms("P7:0:96", ("B", "HL:0:48", "P7:0:48"), ("B", "HL:0:48", "P7:48:96"))
        mms("P6:0:6", *rowsum("Z1", "HL"))
        mms("P3:64:112", ("B", "HL:0:48"), ("B", "HL:48:96"))
        mms("P2:64:112", ("ID", "RI"), ("ID", "RVi"), ("B2N", "Mm"), ("BF", "M1:96:144"))
        act("CKk", "P2:64:112", Fn.Copy)
        tt("KM", "P2:64:112", "WM:0:48", MUL)
        for k in range(3):
            act(R("jk2", 16 * k, 16 * k + 16), R("KM", 16 * k, 16 * k + 16), Fn.Identity, bias=col("IV", k), acc=col("kw", k))
        mms("P0:0:3", ("ID16", "sob"), *rowsum("ZP", "OH"))
        act("swn", "P0:0:3", Fn.Copy, scale=-1.0, bias=-4096.0)
        cp("sl16:0:3", "P0:0:3")
        act("tg", (OWN(t, 0, S + 16), "sl16:0:3"), Fn.Copy)
        cp("qO:0:3", "P6:3:6")
        ts("qO:3:6", "P6:3:6", float(E2), ADD)
        ts("sel", "P7:0:96", "P256", EQ)
        act("WS", "P6:3:6", Fn.Copy, scale=-1.0)
        tt("ncw", "WS", "P6:0:3", SUB)
        tt("T2", ("UE", "qO:0:6"), "sel", MUL)
        mms("P5:64:160", ("BF", "T2"))
        tt("em", "P5:64:160", "WM", MUL)
        for k in range(3):
            tr(col("ew", k), R("em", 16 * k, 16 * k + 16), ADD)
            act(R("jk2", 64 + 16 * k, 80 + 16 * k), R("em", 48 + 16 * k, 64 + 16 * k), Fn.Copy, acc=col("ew", 3 + k))
        ts("OFF:0:3", "ncw", -1.0, MUL, -6.0, ADD)
        cp("OFF:3:9", "ew")
        for k in range(3):
            act(R("TK", 48 * k, 48 * k + 48), "P3:64:112", Fn.Abs, bias=col("ncw", k))
        i = mms("P1:0:144", *[("IDF", "CKk", R("P1", 48 * k, 48 * k + 48)) for k in range(3)], stop=False)
        mms("P1:0:144", ("IDB", "TK"), start=False, dep=(i,))
        for k in range(3):
            act(R("junk", 64 * k, 64 * k + 48), R("P1", 48 * k, 48 * k + 48), Fn.Relu, scale=-1.0, bias=col("kw", k), acc=col("lose", k))
        act("CB:2:5", "lose", Fn.Relu, scale=-1.0, bias=1.0)
        mms("P3:0:1", ("B", "CB:2"), ("B", "CB:3"), ("B", "CB:4"))
        mms("P2:0:3", ("TS", "CB:2:5"), ("NB", "CB:1:4"), ("NB", "CB:0:3"))
        mms("P0:8:11", ("TS2", "CB:2:5"), ("NB", "CB:1:4"), ("NB", "CB:0:3"))
        cn = R("CN", 4 * t, 4 * t + 3)
        ts(sub(cn, 0, 2), "K2", "P3:0:1", MUL)
        ts(sub(cn, 2, 3), "P3:0:1", -1.0, MUL, 48.0, ADD)
        n1, n2 = R("CNL", 8 * t, 8 * t + 3), R("CNL", 8 * t + 4, 8 * t + 7)
        send("cn%d" % t, [transfer(far, fe, "cn%d" % t, cn, n2), transfer(mate, me, "cn%d" % t, cn, n1)], cn, R("CNL", 8 * t, 8 * t + 8))
        act("GX", ("X", "OFF:0:9"), Fn.Copy)
        act("GN", "GX", Fn.Relu, scale=-1.0)
        mms("P4:64:208", ("ID", "GX"), ("B0", "GN"))
        tt("vv", "P2:0:3", "RC", MAX)
        for b in range(3):
            ts(R("DL", 3 * b, 3 * b + 3), "vv", -1.0, MUL, 1024.0 + CAP * b, ADD)
        ts("GV", "P4:64:208", 255.0, MIN)
        snd = R("SND", SNDW * t, SNDW * t + SNDW)
        scatter(snd, "DL:0:9", "GV")
        send("ar%d" % t, [transfer(far, fe[:half], "ar%d" % t, sub(snd, 48, 96), ARP(t, 48, 96)),
                          transfer(far, fe[half:], "ar%d" % t, sub(snd, 96, 144), ARP(t, 96, 144)),
                          transfer(mate, me, "ar%d" % t, sub(snd, 0, 48), ARP(t, 0, 48))], snd, ARP(t, 0, 144))
        scatter(OWN(t, S, OWNW), "DL:0:3", "tg")
        tt("pos", "P0:8:11", "swn", SUB)
        tt("npos", "swn", "P0:8:11", SUB)
        ts("posl", "pos", 15, AND)
        cp("PF", "posl")
        terms = []
        for k in range(3):
            for j, (tab, f, io) in enumerate((("AG", GE, "IA"), ("AGp", LT, "IB"))):
                l, r = R("LL", 128 * (2 * k + j), 128 * (2 * k + j + 1)), R("SS", 64 * (2 * k + j), 64 * (2 * k + j + 1))
                ts(l, tab, col("PF", k), f, 0.5, MUL)
                act(r, io, Fn.Sign, bias=col("npos", k))
                terms.append((l, r))
        i = mms("P7:128:192", ("IDF", "SL24"), stop=False)
        mms("P7:128:192", *terms, start=False, dep=(i,))
        cp("LR", "P7:128:192")
        cp(ARP(t, 144, 656), (OWN(t, 0, S + CAP), "LR:0:32"))
        act(ARP(t, 656, ARPW), (OWN(t, 0, S + CAP), "LR:32:64"), Fn.Copy)
        ts("CE:0:3", "ncw", -1.0, MUL, -16.0, ADD)
        ts("CE:3:6", "ew:3:6", 1.0, ADD)
        ts("CE:6:12", "CE:0:6", 255, AND)
        ts("CE:12:18", "CE:0:6", 0x1F00, AND)
        ts("CFl", "CE:6:12", -1.0, MUL, 0.5, ADD)
        tt("CFh", "CE:12:18", "IV", ADD)
        terms = [("ID8", "ONP")]
        for k in range(6):
            l, lg, r = R("LH", 128 * k, 128 * k + 128), R("LG", 128 * k, 128 * k + 128), R("RH", 256 * k, 256 * k + 256)
            act(r, "IO", Fn.Sign, bias=col("CFl", k))
            act(lg, "AG8", Fn.Sign, scale=-1.0, bias=col("CFh", k))
            ts(l, "AG8", col("CFh", k), EQ, -4096.0 if k < 3 else 4096.0, MUL)
            terms += [(lg, "ONP" if k < 3 else "ONN"), (l, r)]
        i = mms("P5:256:512", *terms[:7], stop=False)
        mms("P5:256:512", *terms[7:], start=False, dep=(i,))
        tt("R0", "R0", "P5:256:512", MIN)
        if t < RO - 1:
            dma("Y", "dM%d" % t, T.X[0:128:16, :], T.R0[:], [R("R0")], [R("X")])
        act(R("FY", 256 * t, 256 * t + 256), "R0", Fn.Sign, scale=-1.0, bias=-0.5)
        ts("L2:10:65", "SLW:9:64", col(n1, 0), SUB, col(n2, 1), SUB)
        ts("s1", "SLW:0:9", col(n1, 0), SUB)
        ts("HT:0:9", "SLW:0:9", col(n1, 0), GE, col(n1, 2), MUL)
        ts("HT:16:25", "s1", col(n2, 0), GE, col(n2, 2), MUL)
        ts("HT:32:41", "s1", col(n2, 1), GE, col(n2, 2), MUL)
        mms("P1:256:265", *[("ID", x) for x in ("SLb:0:9", "HT:0:9", "HT:16:25", "HT:32:41")])
        cp("L2:0:9", "P1:256:265")
        parts = ((144, 592, ARP(t, 144, ARPW), "L2:10:38"), (592, S, ARP(t, 144, ARPW), "L2:38:65"), (0, 144, ARP(t, 0, 288), "L2:0:9"))
        if t < RO - 1:
            tables()
            for j, (lo, hi, win, l) in enumerate(parts):
                if j == 1:
                    act(OWN(t + 1, lo, hi), (win, l), Fn.Copy)
                else:
                    cp(OWN(t + 1, lo, hi), (win, l))
        else:
            mms("P6:0:256", ("Y1", "FY:0:256"), ("Y1", "FY:256:512"), ("Y3", "FY:512:768"))
            act("yct", "P6:0:256", Fn.Copy, bias=0.5)
            dma("Y", "dC", T.yc[:, :], v("yct"), [R("yct")], [])
            for j, (lo, hi, win, l) in enumerate(parts):
                if j == 1:
                    act(R("YG", lo, hi), (win, l), Fn.Copy, scale=-1.0, bias=255.0)
                else:
                    ts(R("YG", lo, hi), (win, l), -1.0, MUL, 255.0, ADD)
                dma("S" if j == 1 else "Y", "dY%d" % j, T.yg[:, lo:hi], T.YG[:, lo:hi], [R("YG", lo, hi)], [])
    emit()
    g.wait_ge(T.sem.lsem, 2 * RO * sent)
    for e, n in list(cnt.items()) + [(d, 16) for d in LOADS]:
        g.wait_ge(T.sem["s" + e if e in cnt else e], n)
